import numpy as np
import ml_dtypes


def mxq(x, axis, fmt="e4m3"):
    dtype, down = {"e4m3": (ml_dtypes.float8_e4m3fn, 7), "e5m2": (ml_dtypes.float8_e5m2, 14)}[fmt]
    v = np.moveaxis(np.asarray(x, np.float32).astype(ml_dtypes.bfloat16).astype(np.float64), axis, -1)
    blocks = v.reshape(v.shape[:-1] + (-1, 32))
    amax = np.abs(blocks).max(-1, keepdims=True)
    byte = np.maximum(np.where(amax > 0, np.frexp(amax)[1] - 1 + 127, 0) - down, 1)
    scale = np.exp2(byte - 127.0)
    codes = (blocks / scale).astype(np.float32).astype(dtype).astype(np.float64)
    return np.moveaxis((codes * scale).reshape(v.shape), -1, axis)


WIDE = False


def mx_kscale(k):
    if not WIDE:
        return np.ones(k)
    levels = np.array([10, -10, 5, -5, 0])
    if k % 512:
        return np.exp2(np.random.permutation(np.resize(levels, k // 32))).repeat(32)
    a = np.empty((k // 512, 16))
    for p in range(k // 512):
        a[p, :8] = np.random.permutation(np.resize(levels, 8))
        for g in range(8):
            far = levels[np.abs(levels - a[p, g]) >= 10]
            a[p, g + 8] = far[np.random.randint(len(far))]
    return np.exp2(a.ravel()).repeat(32)


def f64(x):
    return np.asarray(x).astype(np.float64)


def striped(idx):
    return np.tile(idx.reshape(-1, 16).T, (8, 1)).astype(np.uint16)


def unstriped(offs):
    return offs[:16].T.reshape(-1).astype(np.int64)


def pack_weight(w):
    k, n = w.shape
    w = f64(np.asarray(w, np.float32).astype(ml_dtypes.bfloat16)).reshape(k // 32, 32, n)
    amax = np.abs(w).max(1)
    byte = np.clip(np.where(amax > 0, np.frexp(amax)[1] - 1 + 127 - 7, 1), 1, 254)
    scaled = (w * np.exp2(127.0 - byte)[:, None, :]).reshape(k, n).astype(np.float32)
    words = np.ascontiguousarray(scaled.reshape(k // 512, 128, 4, n).transpose(0, 1, 3, 2)).astype(ml_dtypes.float8_e4m3fn).view(np.uint8)
    return words, np.ascontiguousarray(byte.astype(np.uint8).reshape(k // 512, 16, n))


def unpack_weight(words, scales):
    g, p, n, _ = words.shape
    vals = np.ascontiguousarray(words).view(ml_dtypes.float8_e4m3fn).astype(np.float64) * np.repeat(np.exp2(scales.astype(np.float64) - 127.0), 8, axis=1)[..., None]
    return vals.transpose(0, 1, 3, 2).reshape(g * 512, n)


def gelu(v):
    return 0.5 * v * (1.0 + np.tanh(np.sqrt(2.0 / np.pi) * (v + 0.044715 * v**3)))


K, T, S, H, N = 512, 1024, 512, 512, 128


def setup_inputs():
    n = np.random.standard_normal
    s = mx_kscale(K)[:, None]
    u = mx_kscale(H)
    packed_w2 = pack_weight(n((H, N)) / np.sqrt(H) / u[:, None])
    return {
        "xT": (n((K, T)) * s).astype(np.float32),
        "w1": (n((K, H)) / np.sqrt(K) / s * u).astype(np.float32),
        "w2_words": packed_w2[0],
        "w2_scales": packed_w2[1],
        "pe": (0.5 * n((H, T)) * u[:, None]).astype(np.float32),
        "offs": striped(np.random.permutation(T)[:S]),
    }


def reference(xT, w1, w2_words, w2_scales, pe, offs):
    xq = mxq(f64(xT)[:, unstriped(offs)], 0, "e4m3")
    g = f64(pe)[:, unstriped(offs)]
    h = gelu((mxq(f64(w1), 0, "e4m3").T @ xq) + g)
    return unpack_weight(w2_words, w2_scales).T @ mxq(h, 0, "e4m3")

@@ -1,0 +1,163 @@
+from contextlib import ExitStack
+
+import concourse.mybir as mybir
+
+K, T, S, H, N = 512, 1024, 512, 512, 128
+FLOPS = 2 * K * H * S + 2 * H * N * S
+
+F32 = mybir.dt.float32
+BF16 = mybir.dt.bfloat16
+I32 = mybir.dt.int32
+U32 = mybir.dt.uint32
+U16 = mybir.dt.uint16
+U8 = mybir.dt.uint8
+FP8X4 = mybir.dt.float8_e4m3fn_x4
+GELU = mybir.ActivationFunctionType.Gelu_apprx_tanh
+ADD = mybir.AluOpType.add
+
+P = 128
+PACK = 4
+LINE = 4
+CHUNK = 128
+CHUNKS = S // CHUNK
+
+
+def tile_picked_posadd_gelu_l_kernel(tc, xT, w1, w2_words, w2_scales, pe, offs, out):
+    nc = tc.nc
+    with ExitStack() as ctx:
+        keep = ctx.enter_context(tc.tile_pool(name="keep", bufs=1))
+        psum = ctx.enter_context(tc.psum_pool(name="psum", bufs=1))
+
+        x_rows = xT.rearrange("(p j) c -> p j c", j=PACK)
+        w1_rows = w1.rearrange("(p j) c -> p j c", j=PACK)
+        pe_rows = pe.rearrange("(p t) c -> p t c", t=PACK)
+
+        offsets = keep.tile([P, S // 16], U16, name="offsets")
+        x_raw = [[keep.tile([P, 2, T // 2], F32, name="x_raw%d%d" % (u, h)) for h in range(2)] for u in range(2)]
+        w1_raw = [keep.tile([P, PACK, H // 2], F32, name="w1_raw%d" % h) for h in range(2)]
+        pe_raw = [keep.tile([P, T], F32, name="pe_raw%d" % t) for t in range(PACK)]
+        w2_codes = keep.tile([P, N], U32, name="w2_codes", align_bytes=64)
+        w2_plane = keep.tile([P, N], U8, name="w2_plane", align_bytes=64)
+
+        nc.gpsimd.memset(w2_plane[:].bitcast(I32), 0)
+
+        def load_x(u, h):
+            nc.sync.dma_start(out=x_raw[u][h][:], in_=x_rows[:, 2 * u : 2 * u + 2, h * (T // 2) : (h + 1) * (T // 2)])
+
+        load_x(0, 0)
+        nc.sync.dma_start(offsets[:], offs)
+        load_x(0, 1)
+        load_x(1, 0)
+        load_x(1, 1)
+        for t in (0, 1):
+            nc.sync.dma_start(out=pe_raw[t][:], in_=pe_rows[:, t, :])
+        for h in range(2):
+            nc.sync.dma_start(out=w1_raw[h][:], in_=w1_rows[:, :, h * (H // 2) : (h + 1) * (H // 2)])
+        for t in (2, 3):
+            nc.sync.dma_start(out=pe_raw[t][:], in_=pe_rows[:, t, :])
+        nc.sync.dma_start(out=w2_codes[:].bitcast(I32), in_=w2_words[0].rearrange("p n r -> p (n r)").bitcast(I32))
+        for q in range(4):
+            nc.sync.dma_start(out=w2_plane[32 * q : 32 * q + 4, :].bitcast(I32), in_=w2_scales[0, 4 * q : 4 * q + 4, :].bitcast(I32))
+
+        x_pairs = [keep.tile([P, 2 * T], BF16, name="x_pairs%d" % u) for u in range(2)]
+        x_picked = keep.tile([P, 2, S], U32, name="x_picked")
+        for u in range(2):
+            for h in range(2):
+                dst = x_pairs[u][:, h * T : (h + 1) * T].rearrange("p (c i e) -> p c e i", i=LINE, e=2)
+                src = x_raw[u][h][:].rearrange("p e (c i) -> p c e i", i=LINE)
+                if h == 0:
+                    nc.scalar.copy(out=dst, in_=src)
+                else:
+                    nc.vector.tensor_copy(out=dst, in_=src)
+            nc.vector.tensor_copy(out=x_picked[:, u, :], in_=x_pairs[u][:].bitcast(U32).indirect(offsets[:]))
+        x_woven = keep.tile([P, PACK * S], BF16, name="x_woven", align_bytes=64)
+        nc.scalar.copy(
+            out=x_woven[:].bitcast(U32).rearrange("p (c i u) -> p c u i", i=LINE, u=2),
+            in_=x_picked[:].rearrange("p u (c i) -> p c u i", i=LINE),
+        )
+        pe_picked = keep.tile([P, PACK, S], F32, name="pe_picked")
+        nc.vector.tensor_copy(out=pe_picked[:, 0, :], in_=pe_raw[0][:].indirect(offsets[:]))
+        x_codes = keep.tile([P, S], U32, name="x_codes", align_bytes=64)
+        x_plane = keep.tile([P, S], U8, name="x_plane", align_bytes=64)
+        nc.vector.quantize_mx(out=x_codes[:].bitcast(FP8X4), scales=x_plane[:], in_=x_woven[:])
+        nc.vector.tensor_copy(out=pe_picked[:, 1, :], in_=pe_raw[1][:].indirect(offsets[:]))
+
+        half = P // 2
+        w1_codes = keep.tile([P, H], U32, name="w1_codes", align_bytes=64)
+        w1_plane = keep.tile([P, H], U8, name="w1_plane", align_bytes=64)
+
+        def deal_w1(h, t0, t1, engine_copy):
+            dealt = keep.tile([P, t1 - t0, half * PACK], BF16, name="w1_dealt%d%d" % (h, t0), align_bytes=64)
+            engine_copy(
+                out=dealt[:].rearrange("p t (m j) -> p m j t", j=PACK),
+                in_=w1_raw[h][:].rearrange("p j (m t) -> p m j t", t=PACK)[:, :, :, t0:t1],
+            )
+            return dealt
+
+        def quantise_w1(h, t0, t1, dealt):
+            for t in range(t0, t1):
+                cols = slice(t * P + h * half, t * P + (h + 1) * half)
+                nc.vector.quantize_mx(out=w1_codes[:, cols].bitcast(FP8X4), scales=w1_plane[:, cols], in_=dealt[:, t - t0, :])
+
+        first = deal_w1(0, 0, 4, nc.scalar.copy)
+        low = deal_w1(1, 0, 2, nc.vector.tensor_copy)
+        high = deal_w1(1, 2, 4, nc.scalar.copy)
+        quantise_w1(0, 0, 4, first)
+        quantise_w1(1, 0, 2, low)
+        quantise_w1(1, 2, 4, high)
+
+        nc.vector.tensor_copy(out=pe_picked[:, 2, :], in_=pe_raw[2][:].indirect(offsets[:]))
+
+        acc = [psum.tile([P, PACK, CHUNK], F32, name="acc%d" % c) for c in range(CHUNKS)]
+        for c in range(CHUNKS):
+            cols = slice(c * CHUNK, (c + 1) * CHUNK)
+            for t in range(PACK):
+                rows = slice(t * P, (t + 1) * P)
+                nc.tensor.matmul_mx(
+                    out=acc[c][:, t, :],
+                    lhsT=w1_codes[:, rows].bitcast(FP8X4),
+                    lhsT_scale=w1_plane[:, rows],
+                    rhs=x_codes[:, cols].bitcast(FP8X4),
+                    rhs_scale=x_plane[:, cols],
+                    start=True,
+                    stop=True,
+                )
+
+        hidden = [keep.tile([P, PACK * CHUNK], BF16, name="hidden%d" % c, align_bytes=64) for c in range(CHUNKS)]
+
+        def first_layer(c):
+            cols = slice(c * CHUNK, (c + 1) * CHUNK)
+            entries = offsets[:, c * (CHUNK // 16) : (c + 1) * (CHUNK // 16)]
+            nc.vector.tensor_copy(out=pe_picked[:, 3, cols], in_=pe_raw[3][:].indirect(entries))
+            summed = keep.tile([P, PACK, CHUNK], F32, name="summed%d" % c)
+            nc.vector.tensor_tensor(out=summed[:], in0=acc[c][:], in1=pe_picked[:, :, cols], op=ADD)
+            nc.scalar.activation(
+                out=hidden[c][:].rearrange("p (c i t) -> p c t i", i=LINE, t=PACK),
+                in_=summed[:].rearrange("p t (c i) -> p c t i", i=LINE),
+                func=GELU,
+            )
+
+        def second_layer(c):
+            cols = slice(c * CHUNK, (c + 1) * CHUNK)
+            h_codes = keep.tile([P, CHUNK], U32, name="h_codes%d" % c, align_bytes=64)
+            h_plane = keep.tile([P, CHUNK], U8, name="h_plane%d" % c, align_bytes=64)
+            nc.vector.quantize_mx(out=h_codes[:].bitcast(FP8X4), scales=h_plane[:], in_=hidden[c][:])
+            result = psum.tile([P, CHUNK], F32, name="result%d" % c)
+            nc.tensor.matmul_mx(
+                out=result[:],
+                lhsT=w2_codes[:].bitcast(FP8X4),
+                lhsT_scale=w2_plane[:],
+                rhs=h_codes[:].bitcast(FP8X4),
+                rhs_scale=h_plane[:],
+                start=True,
+                stop=True,
+            )
+            staged = keep.tile([P, CHUNK], F32, name="staged%d" % c)
+            nc.scalar.copy(out=staged[:], in_=result[:])
+            nc.sync.dma_start(out=out[:, cols], in_=staged[:])
+
+        for c in range(CHUNKS + 1):
+            if c < CHUNKS:
+                first_layer(c)
+            if c > 0:
+                second_layer(c - 1)

@@ -33,22 +33,22 @@ def tile_picked_posadd_gelu_l_kernel(tc, xT, w1, w2_words, w2_scales, pe, offs, 
         pe_rows = pe.rearrange("(p t) c -> p t c", t=PACK)
 
         offsets = keep.tile([P, S // 16], U16, name="offsets")
-        x_raw = [[keep.tile([P, 2, T // 2], F32, name="x_raw%d%d" % (u, h)) for h in range(2)] for u in range(2)]
+        x_raw = [keep.tile([P, T], F32, name="x_raw%d" % j) for j in range(PACK)]
         w1_raw = [keep.tile([P, PACK, H // 2], F32, name="w1_raw%d" % h) for h in range(2)]
         pe_raw = [keep.tile([P, T], F32, name="pe_raw%d" % t) for t in range(PACK)]
         w2_codes = keep.tile([P, N], U32, name="w2_codes", align_bytes=64)
         w2_plane = keep.tile([P, N], U8, name="w2_plane", align_bytes=64)
 
         nc.gpsimd.memset(w2_plane[:].bitcast(I32), 0)
+        warm_in = keep.tile([P, 1], F32, name="warm_in")
+        warm_out = keep.tile([P, 1], F32, name="warm_out")
+        nc.gpsimd.memset(warm_in[:], 0.0)
+        nc.scalar.activation(out=warm_out[:], in_=warm_in[:], func=GELU)
 
-        def load_x(u, h):
-            nc.sync.dma_start(out=x_raw[u][h][:], in_=x_rows[:, 2 * u : 2 * u + 2, h * (T // 2) : (h + 1) * (T // 2)])
-
-        load_x(0, 0)
-        nc.sync.dma_start(offsets[:], offs)
-        load_x(0, 1)
-        load_x(1, 0)
-        load_x(1, 1)
+        for j in range(PACK):
+            nc.sync.dma_start(out=x_raw[j][:], in_=x_rows[:, j, :])
+            if j == 0:
+                nc.sync.dma_start(offsets[:], offs)
         for t in (0, 1):
             nc.sync.dma_start(out=pe_raw[t][:], in_=pe_rows[:, t, :])
         for h in range(2):
@@ -59,28 +59,33 @@ def tile_picked_posadd_gelu_l_kernel(tc, xT, w1, w2_words, w2_scales, pe, offs, 
         for q in range(4):
             nc.sync.dma_start(out=w2_plane[32 * q : 32 * q + 4, :].bitcast(I32), in_=w2_scales[0, 4 * q : 4 * q + 4, :].bitcast(I32))
 
-        x_pairs = [keep.tile([P, 2 * T], BF16, name="x_pairs%d" % u) for u in range(2)]
-        x_picked = keep.tile([P, 2, S], U32, name="x_picked")
-        for u in range(2):
-            for h in range(2):
-                dst = x_pairs[u][:, h * T : (h + 1) * T].rearrange("p (c i e) -> p c e i", i=LINE, e=2)
-                src = x_raw[u][h][:].rearrange("p e (c i) -> p c e i", i=LINE)
-                if h == 0:
-                    nc.scalar.copy(out=dst, in_=src)
-                else:
-                    nc.vector.tensor_copy(out=dst, in_=src)
-            nc.vector.tensor_copy(out=x_picked[:, u, :], in_=x_pairs[u][:].bitcast(U32).indirect(offsets[:]))
+        def entries(lo, hi):
+            return offsets[:, lo // 16 : hi // 16]
+
+        x_picked = keep.tile([P, PACK, S], BF16, name="x_picked")
         x_woven = keep.tile([P, PACK * S], BF16, name="x_woven", align_bytes=64)
-        nc.scalar.copy(
-            out=x_woven[:].bitcast(U32).rearrange("p (c i u) -> p c u i", i=LINE, u=2),
-            in_=x_picked[:].rearrange("p u (c i) -> p c u i", i=LINE),
-        )
-        pe_picked = keep.tile([P, PACK, S], F32, name="pe_picked")
-        nc.vector.tensor_copy(out=pe_picked[:, 0, :], in_=pe_raw[0][:].indirect(offsets[:]))
+
+        def weave(u, lo, hi):
+            nc.scalar.copy(
+                out=x_woven[:, PACK * lo : PACK * hi].rearrange("p (c i u e) -> p u c e i", i=8, u=2, e=2)[:, u],
+                in_=x_picked[:, 2 * u : 2 * u + 2, lo:hi].rearrange("p e (c i) -> p c e i", i=8),
+            )
+
+        for j in range(PACK - 1):
+            nc.vector.tensor_copy(out=x_picked[:, j, :], in_=x_raw[j][:].indirect(offsets[:]))
+            if j == 1:
+                weave(0, 0, S)
+        for lo in (0, S // 2):
+            hi = lo + S // 2
+            nc.vector.tensor_copy(out=x_picked[:, PACK - 1, lo:hi], in_=x_raw[PACK - 1][:].indirect(entries(lo, hi)))
+            weave(1, lo, hi)
+        pe_low = keep.tile([P, 2, S], F32, name="pe_low")
+        pe_high = keep.tile([P, CHUNKS + 2, CHUNK], F32, name="pe_high")
+        nc.vector.tensor_copy(out=pe_low[:, 0, :], in_=pe_raw[0][:].indirect(offsets[:]))
         x_codes = keep.tile([P, S], U32, name="x_codes", align_bytes=64)
         x_plane = keep.tile([P, S], U8, name="x_plane", align_bytes=64)
         nc.vector.quantize_mx(out=x_codes[:].bitcast(FP8X4), scales=x_plane[:], in_=x_woven[:])
-        nc.vector.tensor_copy(out=pe_picked[:, 1, :], in_=pe_raw[1][:].indirect(offsets[:]))
+        nc.vector.tensor_copy(out=pe_low[:, 1, :], in_=pe_raw[1][:].indirect(offsets[:]))
 
         half = P // 2
         w1_codes = keep.tile([P, H], U32, name="w1_codes", align_bytes=64)
@@ -106,43 +111,61 @@ def tile_picked_posadd_gelu_l_kernel(tc, xT, w1, w2_words, w2_scales, pe, offs, 
         quantise_w1(1, 0, 2, low)
         quantise_w1(1, 2, 4, high)
 
-        nc.vector.tensor_copy(out=pe_picked[:, 2, :], in_=pe_raw[2][:].indirect(offsets[:]))
+        nc.vector.tensor_copy(out=pe_high[:, :CHUNKS, :].rearrange("p c s -> p (c s)"), in_=pe_raw[2][:].indirect(offsets[:]))
 
-        acc = [psum.tile([P, PACK, CHUNK], F32, name="acc%d" % c) for c in range(CHUNKS)]
-        for c in range(CHUNKS):
-            cols = slice(c * CHUNK, (c + 1) * CHUNK)
-            for t in range(PACK):
-                rows = slice(t * P, (t + 1) * P)
+        def first_product(name, u, lo, hi):
+            acc = psum.tile([P, 2, hi - lo], F32, name=name)
+            for e in range(2):
+                rows = slice((2 * u + e) * P, (2 * u + e + 1) * P)
                 nc.tensor.matmul_mx(
-                    out=acc[c][:, t, :],
+                    out=acc[:, e, :],
                     lhsT=w1_codes[:, rows].bitcast(FP8X4),
                     lhsT_scale=w1_plane[:, rows],
-                    rhs=x_codes[:, cols].bitcast(FP8X4),
-                    rhs_scale=x_plane[:, cols],
+                    rhs=x_codes[:, lo:hi].bitcast(FP8X4),
+                    rhs_scale=x_plane[:, lo:hi],
                     start=True,
                     stop=True,
                 )
+            return acc
 
-        hidden = [keep.tile([P, PACK * CHUNK], BF16, name="hidden%d" % c, align_bytes=64) for c in range(CHUNKS)]
+        summed = [keep.tile([P, PACK, CHUNK], F32, name="summed%d" % c) for c in range(CHUNKS)]
+        for lo, hi in ((0, CHUNK), (CHUNK, 2 * CHUNK), (2 * CHUNK, S)):
+            acc = first_product("low%d" % lo, 0, lo, hi)
+            drained = keep.tile([P, 2, hi - lo], F32, name="drained%d" % lo)
+            nc.scalar.copy(out=drained[:], in_=acc[:])
+            for at in range(lo, hi, CHUNK):
+                nc.gpsimd.tensor_tensor(
+                    out=summed[at // CHUNK][:, 0:2, :], in0=drained[:, :, at - lo : at - lo + CHUNK], in1=pe_low[:, :, at : at + CHUNK], op=ADD
+                )
+        high = [first_product("high%d" % h, 1, h * (S // 2), (h + 1) * (S // 2)) for h in range(2)]
 
-        def first_layer(c):
-            cols = slice(c * CHUNK, (c + 1) * CHUNK)
-            entries = offsets[:, c * (CHUNK // 16) : (c + 1) * (CHUNK // 16)]
-            nc.vector.tensor_copy(out=pe_picked[:, 3, cols], in_=pe_raw[3][:].indirect(entries))
-            summed = keep.tile([P, PACK, CHUNK], F32, name="summed%d" % c)
-            nc.vector.tensor_tensor(out=summed[:], in0=acc[c][:], in1=pe_picked[:, :, cols], op=ADD)
+        pieces = ((0, 2 * CHUNK), (2 * CHUNK, 3 * CHUNK), (3 * CHUNK, S))
+        hidden = [keep.tile([P, PACK * (hi - lo)], BF16, name="hidden%d" % lo, align_bytes=64) for lo, hi in pieces]
+
+        def pick_last(c):
+            nc.vector.tensor_copy(out=pe_high[:, CHUNKS + c % 2, :], in_=pe_raw[3][:].indirect(entries(c * CHUNK, (c + 1) * CHUNK)))
+
+        def first_layer(c, g):
+            at = c * CHUNK - pieces[g][0]
+            ring = CHUNKS + c % 2
+            nc.vector.tensor_tensor(
+                out=summed[c][:, 2:4, :],
+                in0=high[c // 2][:, :, (c % 2) * CHUNK : (c % 2 + 1) * CHUNK],
+                in1=pe_high[:, c : ring + 1 : ring - c, :],
+                op=ADD,
+            )
             nc.scalar.activation(
-                out=hidden[c][:].rearrange("p (c i t) -> p c t i", i=LINE, t=PACK),
-                in_=summed[:].rearrange("p t (c i) -> p c t i", i=LINE),
+                out=hidden[g][:, PACK * at : PACK * (at + CHUNK)].rearrange("p (c i t) -> p c t i", i=LINE, t=PACK),
+                in_=summed[c][:].rearrange("p t (c i) -> p c t i", i=LINE),
                 func=GELU,
             )
 
-        def second_layer(c):
-            cols = slice(c * CHUNK, (c + 1) * CHUNK)
-            h_codes = keep.tile([P, CHUNK], U32, name="h_codes%d" % c, align_bytes=64)
-            h_plane = keep.tile([P, CHUNK], U8, name="h_plane%d" % c, align_bytes=64)
-            nc.vector.quantize_mx(out=h_codes[:].bitcast(FP8X4), scales=h_plane[:], in_=hidden[c][:])
-            result = psum.tile([P, CHUNK], F32, name="result%d" % c)
+        def second_layer(g):
+            lo, hi = pieces[g]
+            h_codes = keep.tile([P, hi - lo], U32, name="h_codes%d" % g, align_bytes=64)
+            h_plane = keep.tile([P, hi - lo], U8, name="h_plane%d" % g, align_bytes=64)
+            nc.vector.quantize_mx(out=h_codes[:].bitcast(FP8X4), scales=h_plane[:], in_=hidden[g][:])
+            result = psum.tile([P, hi - lo], F32, name="result%d" % g)
             nc.tensor.matmul_mx(
                 out=result[:],
                 lhsT=w2_codes[:].bitcast(FP8X4),
@@ -152,12 +175,14 @@ def tile_picked_posadd_gelu_l_kernel(tc, xT, w1, w2_words, w2_scales, pe, offs, 
                 start=True,
                 stop=True,
             )
-            staged = keep.tile([P, CHUNK], F32, name="staged%d" % c)
+            staged = keep.tile([P, hi - lo], F32, name="staged%d" % g)
             nc.scalar.copy(out=staged[:], in_=result[:])
-            nc.sync.dma_start(out=out[:, cols], in_=staged[:])
+            nc.sync.dma_start(out=out[:, lo:hi], in_=staged[:])
 
-        for c in range(CHUNKS + 1):
-            if c < CHUNKS:
-                first_layer(c)
-            if c > 0:
-                second_layer(c - 1)
+        pick_last(0)
+        for c in range(CHUNKS):
+            if c + 1 < CHUNKS:
+                pick_last(c + 1)
+            first_layer(c, max(c - 1, 0))
+        for g in range(len(pieces)):
+            second_layer(g)

@@ -13,6 +13,7 @@ U16 = mybir.dt.uint16
 U8 = mybir.dt.uint8
 FP8X4 = mybir.dt.float8_e4m3fn_x4
 GELU = mybir.ActivationFunctionType.Gelu_apprx_tanh
+COPY = mybir.ActivationFunctionType.Copy
 ADD = mybir.AluOpType.add
 
 P = 128
@@ -65,27 +66,28 @@ def tile_picked_posadd_gelu_l_kernel(tc, xT, w1, w2_words, w2_scales, pe, offs, 
         x_picked = keep.tile([P, PACK, S], BF16, name="x_picked")
         x_woven = keep.tile([P, PACK * S], BF16, name="x_woven", align_bytes=64)
 
-        def weave(u, lo, hi):
+        def weave(lo, hi):
             nc.scalar.copy(
-                out=x_woven[:, PACK * lo : PACK * hi].rearrange("p (c i u e) -> p u c e i", i=8, u=2, e=2)[:, u],
-                in_=x_picked[:, 2 * u : 2 * u + 2, lo:hi].rearrange("p e (c i) -> p c e i", i=8),
+                out=x_woven[:, PACK * lo : PACK * hi].rearrange("p (c i j) -> p c j i", i=LINE, j=PACK),
+                in_=x_picked[:, :, lo:hi].rearrange("p j (c i) -> p c j i", i=LINE),
             )
 
-        for j in range(PACK - 1):
-            nc.vector.tensor_copy(out=x_picked[:, j, :], in_=x_raw[j][:].indirect(offsets[:]))
-            if j == 1:
-                weave(0, 0, S)
+        x_cast = keep.tile([P, T], BF16, name="x_cast")
+        nc.vector.tensor_copy(out=x_picked[:, 0, :], in_=x_raw[0][:].indirect(offsets[:]))
+        nc.scalar.copy(out=x_cast[:], in_=x_raw[1][:])
+        nc.scalar.activation(out=x_picked[:, 1, :], in_=x_cast[:].indirect(offsets[:]), func=COPY)
+        nc.vector.tensor_copy(out=x_picked[:, 2, :], in_=x_raw[2][:].indirect(offsets[:]))
         for lo in (0, S // 2):
             hi = lo + S // 2
             nc.vector.tensor_copy(out=x_picked[:, PACK - 1, lo:hi], in_=x_raw[PACK - 1][:].indirect(entries(lo, hi)))
-            weave(1, lo, hi)
+            weave(lo, hi)
         pe_low = keep.tile([P, 2, S], F32, name="pe_low")
         pe_high = keep.tile([P, CHUNKS + 2, CHUNK], F32, name="pe_high")
         nc.vector.tensor_copy(out=pe_low[:, 0, :], in_=pe_raw[0][:].indirect(offsets[:]))
         x_codes = keep.tile([P, S], U32, name="x_codes", align_bytes=64)
         x_plane = keep.tile([P, S], U8, name="x_plane", align_bytes=64)
-        nc.vector.quantize_mx(out=x_codes[:].bitcast(FP8X4), scales=x_plane[:], in_=x_woven[:])
         nc.vector.tensor_copy(out=pe_low[:, 1, :], in_=pe_raw[1][:].indirect(offsets[:]))
+        nc.vector.quantize_mx(out=x_codes[:].bitcast(FP8X4), scales=x_plane[:], in_=x_woven[:])
 
         half = P // 2
         w1_codes = keep.tile([P, H], U32, name="w1_codes", align_bytes=64)

@@ -13,12 +13,10 @@ U16 = mybir.dt.uint16
 U8 = mybir.dt.uint8
 FP8X4 = mybir.dt.float8_e4m3fn_x4
 GELU = mybir.ActivationFunctionType.Gelu_apprx_tanh
-COPY = mybir.ActivationFunctionType.Copy
 ADD = mybir.AluOpType.add
 
 P = 128
 PACK = 4
-LINE = 4
 CHUNK = 128
 CHUNKS = S // CHUNK
 
@@ -35,7 +33,7 @@ def tile_picked_posadd_gelu_l_kernel(tc, xT, w1, w2_words, w2_scales, pe, offs, 
 
         offsets = keep.tile([P, S // 16], U16, name="offsets")
         x_raw = [keep.tile([P, T], F32, name="x_raw%d" % j) for j in range(PACK)]
-        w1_raw = [keep.tile([P, PACK, H // 2], F32, name="w1_raw%d" % h) for h in range(2)]
+        w1_raw = keep.tile([P, PACK, H], F32, name="w1_raw")
         pe_raw = [keep.tile([P, T], F32, name="pe_raw%d" % t) for t in range(PACK)]
         w2_codes = keep.tile([P, N], U32, name="w2_codes", align_bytes=64)
         w2_plane = keep.tile([P, N], U8, name="w2_plane", align_bytes=64)
@@ -50,11 +48,8 @@ def tile_picked_posadd_gelu_l_kernel(tc, xT, w1, w2_words, w2_scales, pe, offs, 
             nc.sync.dma_start(out=x_raw[j][:], in_=x_rows[:, j, :])
             if j == 0:
                 nc.sync.dma_start(offsets[:], offs)
-        for t in (0, 1):
-            nc.sync.dma_start(out=pe_raw[t][:], in_=pe_rows[:, t, :])
-        for h in range(2):
-            nc.sync.dma_start(out=w1_raw[h][:], in_=w1_rows[:, :, h * (H // 2) : (h + 1) * (H // 2)])
-        for t in (2, 3):
+        nc.sync.dma_start(out=w1_raw[:], in_=w1_rows)
+        for t in range(PACK):
             nc.sync.dma_start(out=pe_raw[t][:], in_=pe_rows[:, t, :])
         nc.sync.dma_start(out=w2_codes[:].bitcast(I32), in_=w2_words[0].rearrange("p n r -> p (n r)").bitcast(I32))
         for q in range(4):
@@ -66,101 +61,81 @@ def tile_picked_posadd_gelu_l_kernel(tc, xT, w1, w2_words, w2_scales, pe, offs, 
         x_picked = keep.tile([P, PACK, S], BF16, name="x_picked")
         x_woven = keep.tile([P, PACK * S], BF16, name="x_woven", align_bytes=64)
 
-        def weave(lo, hi):
-            nc.scalar.copy(
-                out=x_woven[:, PACK * lo : PACK * hi].rearrange("p (c i j) -> p c j i", i=LINE, j=PACK),
-                in_=x_picked[:, :, lo:hi].rearrange("p j (c i) -> p c j i", i=LINE),
+        def weave(engine_copy, u, lo, hi):
+            engine_copy(
+                out=x_woven[:, PACK * lo : PACK * hi].rearrange("p (s j) -> p s j", j=PACK)[:, :, 2 * u : 2 * u + 2],
+                in_=x_picked[:, 2 * u : 2 * u + 2, lo:hi].rearrange("p j s -> p s j"),
             )
 
-        x_cast = keep.tile([P, T], BF16, name="x_cast")
-        nc.vector.tensor_copy(out=x_picked[:, 0, :], in_=x_raw[0][:].indirect(offsets[:]))
-        nc.scalar.copy(out=x_cast[:], in_=x_raw[1][:])
-        nc.scalar.activation(out=x_picked[:, 1, :], in_=x_cast[:].indirect(offsets[:]), func=COPY)
-        nc.vector.tensor_copy(out=x_picked[:, 2, :], in_=x_raw[2][:].indirect(offsets[:]))
-        for lo in (0, S // 2):
+        for j in range(PACK - 1):
+            nc.vector.tensor_copy(out=x_picked[:, j, :], in_=x_raw[j][:].indirect(offsets[:]))
+        weave(nc.scalar.copy, 0, 0, S)
+        for lo, engine_copy in ((0, nc.scalar.copy), (S // 2, nc.vector.tensor_copy)):
             hi = lo + S // 2
             nc.vector.tensor_copy(out=x_picked[:, PACK - 1, lo:hi], in_=x_raw[PACK - 1][:].indirect(entries(lo, hi)))
-            weave(lo, hi)
-        pe_low = keep.tile([P, 2, S], F32, name="pe_low")
-        pe_high = keep.tile([P, CHUNKS + 2, CHUNK], F32, name="pe_high")
-        nc.vector.tensor_copy(out=pe_low[:, 0, :], in_=pe_raw[0][:].indirect(offsets[:]))
+            weave(engine_copy, 1, lo, hi)
         x_codes = keep.tile([P, S], U32, name="x_codes", align_bytes=64)
         x_plane = keep.tile([P, S], U8, name="x_plane", align_bytes=64)
-        nc.vector.tensor_copy(out=pe_low[:, 1, :], in_=pe_raw[1][:].indirect(offsets[:]))
-        nc.vector.quantize_mx(out=x_codes[:].bitcast(FP8X4), scales=x_plane[:], in_=x_woven[:])
+        for lo in (0, S // 2):
+            hi = lo + S // 2
+            nc.vector.quantize_mx(out=x_codes[:, lo:hi].bitcast(FP8X4), scales=x_plane[:, lo:hi], in_=x_woven[:, PACK * lo : PACK * hi])
 
-        half = P // 2
-        w1_codes = keep.tile([P, H], U32, name="w1_codes", align_bytes=64)
-        w1_plane = keep.tile([P, H], U8, name="w1_plane", align_bytes=64)
-
-        def deal_w1(h, t0, t1, engine_copy):
-            dealt = keep.tile([P, t1 - t0, half * PACK], BF16, name="w1_dealt%d%d" % (h, t0), align_bytes=64)
+        w1_codes = [keep.tile([P, 2 * P], U32, name="w1_codes%d" % u, align_bytes=64) for u in range(2)]
+        w1_plane = [keep.tile([P, 2 * P], U8, name="w1_plane%d" % u, align_bytes=64) for u in range(2)]
+        dealt = [keep.tile([P, 2 * P * PACK], BF16, name="w1_dealt%d" % u, align_bytes=64) for u in range(2)]
+        for u, engine_copy in enumerate((nc.vector.tensor_copy, nc.scalar.copy)):
             engine_copy(
-                out=dealt[:].rearrange("p t (m j) -> p m j t", j=PACK),
-                in_=w1_raw[h][:].rearrange("p j (m t) -> p m j t", t=PACK)[:, :, :, t0:t1],
+                out=dealt[u][:].rearrange("p (t m j) -> p m j t", t=2, j=PACK),
+                in_=w1_raw[:].rearrange("p j (m t) -> p m j t", t=PACK)[:, :, :, 2 * u : 2 * u + 2],
             )
-            return dealt
+        for u in range(2):
+            nc.vector.quantize_mx(out=w1_codes[u][:].bitcast(FP8X4), scales=w1_plane[u][:], in_=dealt[u][:])
 
-        def quantise_w1(h, t0, t1, dealt):
-            for t in range(t0, t1):
-                cols = slice(t * P + h * half, t * P + (h + 1) * half)
-                nc.vector.quantize_mx(out=w1_codes[:, cols].bitcast(FP8X4), scales=w1_plane[:, cols], in_=dealt[:, t - t0, :])
+        pe_first = keep.tile([P, S], F32, name="pe_first")
+        nc.vector.tensor_copy(out=pe_first[:], in_=pe_raw[0][:].indirect(offsets[:]))
 
-        first = deal_w1(0, 0, 4, nc.scalar.copy)
-        low = deal_w1(1, 0, 2, nc.vector.tensor_copy)
-        high = deal_w1(1, 2, 4, nc.scalar.copy)
-        quantise_w1(0, 0, 4, first)
-        quantise_w1(1, 0, 2, low)
-        quantise_w1(1, 2, 4, high)
-
-        nc.vector.tensor_copy(out=pe_high[:, :CHUNKS, :].rearrange("p c s -> p (c s)"), in_=pe_raw[2][:].indirect(offsets[:]))
-
-        def first_product(name, u, lo, hi):
-            acc = psum.tile([P, 2, hi - lo], F32, name=name)
-            for e in range(2):
-                rows = slice((2 * u + e) * P, (2 * u + e + 1) * P)
-                nc.tensor.matmul_mx(
-                    out=acc[:, e, :],
-                    lhsT=w1_codes[:, rows].bitcast(FP8X4),
-                    lhsT_scale=w1_plane[:, rows],
-                    rhs=x_codes[:, lo:hi].bitcast(FP8X4),
-                    rhs_scale=x_plane[:, lo:hi],
-                    start=True,
-                    stop=True,
-                )
+        def first_product(t, lo, hi):
+            acc = psum.tile([P, hi - lo], F32, name="acc%d_%d" % (t, lo))
+            rows = slice((t % 2) * P, (t % 2 + 1) * P)
+            nc.tensor.matmul_mx(
+                out=acc[:],
+                lhsT=w1_codes[t // 2][:, rows].bitcast(FP8X4),
+                lhsT_scale=w1_plane[t // 2][:, rows],
+                rhs=x_codes[:, lo:hi].bitcast(FP8X4),
+                rhs_scale=x_plane[:, lo:hi],
+                start=True,
+                stop=True,
+            )
             return acc
 
-        summed = [keep.tile([P, PACK, CHUNK], F32, name="summed%d" % c) for c in range(CHUNKS)]
-        for lo, hi in ((0, CHUNK), (CHUNK, 2 * CHUNK), (2 * CHUNK, S)):
-            acc = first_product("low%d" % lo, 0, lo, hi)
-            drained = keep.tile([P, 2, hi - lo], F32, name="drained%d" % lo)
-            nc.scalar.copy(out=drained[:], in_=acc[:])
-            for at in range(lo, hi, CHUNK):
-                nc.gpsimd.tensor_tensor(
-                    out=summed[at // CHUNK][:, 0:2, :], in0=drained[:, :, at - lo : at - lo + CHUNK], in1=pe_low[:, :, at : at + CHUNK], op=ADD
-                )
-        high = [first_product("high%d" % h, 1, h * (S // 2), (h + 1) * (S // 2)) for h in range(2)]
+        summed = keep.tile([P, PACK, S], F32, name="summed")
+        drained = keep.tile([P, PACK - 1, S], F32, name="drained")
+
+        def pick_and_add(t, lo, hi):
+            nc.vector.tensor_tensor(
+                out=summed[:, t, lo:hi], in0=pe_raw[t][:].indirect(entries(lo, hi)), in1=drained[:, t - 1, lo:hi], op=ADD
+            )
+
+        nc.vector.tensor_tensor(out=summed[:, 0, :], in0=first_product(0, 0, S)[:], in1=pe_first[:], op=ADD)
+        for t, lo, hi in ((1, 0, S // 2), (1, S // 2, S), (2, 0, S), (3, 0, S)):
+            nc.scalar.copy(out=drained[:, t - 1, lo:hi], in_=first_product(t, lo, hi)[:])
+            if t < PACK - 1:
+                pick_and_add(t, lo, hi)
 
         pieces = ((0, 2 * CHUNK), (2 * CHUNK, 3 * CHUNK), (3 * CHUNK, S))
         hidden = [keep.tile([P, PACK * (hi - lo)], BF16, name="hidden%d" % lo, align_bytes=64) for lo, hi in pieces]
 
-        def pick_last(c):
-            nc.vector.tensor_copy(out=pe_high[:, CHUNKS + c % 2, :], in_=pe_raw[3][:].indirect(entries(c * CHUNK, (c + 1) * CHUNK)))
-
-        def first_layer(c, g):
-            at = c * CHUNK - pieces[g][0]
-            ring = CHUNKS + c % 2
-            nc.vector.tensor_tensor(
-                out=summed[c][:, 2:4, :],
-                in0=high[c // 2][:, :, (c % 2) * CHUNK : (c % 2 + 1) * CHUNK],
-                in1=pe_high[:, c : ring + 1 : ring - c, :],
-                op=ADD,
-            )
+        def gelu_pair(u, g, lo, hi):
+            at = pieces[g][0]
             nc.scalar.activation(
-                out=hidden[g][:, PACK * at : PACK * (at + CHUNK)].rearrange("p (c i t) -> p c t i", i=LINE, t=PACK),
-                in_=summed[c][:].rearrange("p t (c i) -> p c t i", i=LINE),
+                out=hidden[g][:, PACK * (lo - at) : PACK * (hi - at)].rearrange("p (s t) -> p s t", t=PACK)[:, :, 2 * u : 2 * u + 2],
+                in_=summed[:, 2 * u : 2 * u + 2, lo:hi].rearrange("p t s -> p s t"),
                 func=GELU,
             )
+
+        def first_layer(c, g):
+            pick_and_add(PACK - 1, c * CHUNK, (c + 1) * CHUNK)
+            gelu_pair(1, g, c * CHUNK, (c + 1) * CHUNK)
 
         def second_layer(g):
             lo, hi = pieces[g]
@@ -181,10 +156,9 @@ def tile_picked_posadd_gelu_l_kernel(tc, xT, w1, w2_words, w2_scales, pe, offs, 
             nc.scalar.copy(out=staged[:], in_=result[:])
             nc.sync.dma_start(out=out[:, lo:hi], in_=staged[:])
 
-        pick_last(0)
+        for g, (lo, hi) in enumerate(pieces):
+            gelu_pair(0, g, lo, hi)
         for c in range(CHUNKS):
-            if c + 1 < CHUNKS:
-                pick_last(c + 1)
             first_layer(c, max(c - 1, 0))
         for g in range(len(pieces)):
             second_layer(g)

@@ -13,6 +13,7 @@ U16 = mybir.dt.uint16
 U8 = mybir.dt.uint8
 FP8X4 = mybir.dt.float8_e4m3fn_x4
 GELU = mybir.ActivationFunctionType.Gelu_apprx_tanh
+COPY = mybir.ActivationFunctionType.Copy
 ADD = mybir.AluOpType.add
 
 P = 128
@@ -28,12 +29,12 @@ def tile_picked_posadd_gelu_l_kernel(tc, xT, w1, w2_words, w2_scales, pe, offs, 
         psum = ctx.enter_context(tc.psum_pool(name="psum", bufs=1))
 
         x_rows = xT.rearrange("(p j) c -> p j c", j=PACK)
-        w1_rows = w1.rearrange("(p j) c -> p j c", j=PACK)
+        w1_rows = w1.rearrange("(p j) c -> p (j c)", j=PACK)
         pe_rows = pe.rearrange("(p t) c -> p t c", t=PACK)
 
         offsets = keep.tile([P, S // 16], U16, name="offsets")
         x_raw = [keep.tile([P, T], F32, name="x_raw%d" % j) for j in range(PACK)]
-        w1_raw = keep.tile([P, PACK, H], F32, name="w1_raw")
+        w1_raw = keep.tile([P, PACK * H], F32, name="w1_raw")
         pe_raw = [keep.tile([P, T], F32, name="pe_raw%d" % t) for t in range(PACK)]
         w2_codes = keep.tile([P, N], U32, name="w2_codes", align_bytes=64)
         w2_plane = keep.tile([P, N], U8, name="w2_plane", align_bytes=64)
@@ -48,7 +49,8 @@ def tile_picked_posadd_gelu_l_kernel(tc, xT, w1, w2_words, w2_scales, pe, offs, 
             nc.sync.dma_start(out=x_raw[j][:], in_=x_rows[:, j, :])
             if j == 0:
                 nc.sync.dma_start(offsets[:], offs)
-        nc.sync.dma_start(out=w1_raw[:], in_=w1_rows)
+        for u in range(2):
+            nc.sync.dma_start(out=w1_raw[:, 2 * u * H : 2 * (u + 1) * H], in_=w1_rows[:, 2 * u * H : 2 * (u + 1) * H])
         for t in range(PACK):
             nc.sync.dma_start(out=pe_raw[t][:], in_=pe_rows[:, t, :])
         nc.sync.dma_start(out=w2_codes[:].bitcast(I32), in_=w2_words[0].rearrange("p n r -> p (n r)").bitcast(I32))
@@ -59,34 +61,37 @@ def tile_picked_posadd_gelu_l_kernel(tc, xT, w1, w2_words, w2_scales, pe, offs, 
             return offsets[:, lo // 16 : hi // 16]
 
         x_picked = keep.tile([P, PACK, S], BF16, name="x_picked")
-        x_woven = keep.tile([P, PACK * S], BF16, name="x_woven", align_bytes=64)
+        halves = ((0, S // 2), (S // 2, S))
+        x_woven = [keep.tile([P, PACK * S // 2], BF16, name="x_woven%d" % h, align_bytes=64) for h in range(2)]
 
-        def weave(engine_copy, u, lo, hi):
+        def weave(engine_copy, u, h):
+            lo, hi = halves[h]
             engine_copy(
-                out=x_woven[:, PACK * lo : PACK * hi].rearrange("p (s j) -> p s j", j=PACK)[:, :, 2 * u : 2 * u + 2],
+                out=x_woven[h][:].rearrange("p (s j) -> p s j", j=PACK)[:, :, 2 * u : 2 * u + 2],
                 in_=x_picked[:, 2 * u : 2 * u + 2, lo:hi].rearrange("p j s -> p s j"),
             )
 
-        for j in range(PACK - 1):
+        x_cast = keep.tile([P, T], BF16, name="x_cast")
+        nc.scalar.copy(out=x_cast[:], in_=x_raw[0][:])
+        nc.scalar.activation(out=x_picked[:, 0, :], in_=x_cast[:].indirect(offsets[:]), func=COPY)
+        for j in range(1, PACK):
             nc.vector.tensor_copy(out=x_picked[:, j, :], in_=x_raw[j][:].indirect(offsets[:]))
-        weave(nc.scalar.copy, 0, 0, S)
-        for lo, engine_copy in ((0, nc.scalar.copy), (S // 2, nc.vector.tensor_copy)):
-            hi = lo + S // 2
-            nc.vector.tensor_copy(out=x_picked[:, PACK - 1, lo:hi], in_=x_raw[PACK - 1][:].indirect(entries(lo, hi)))
-            weave(engine_copy, 1, lo, hi)
+        for u, engine_copy in enumerate((nc.scalar.copy, nc.vector.tensor_copy)):
+            for h in range(2):
+                weave(engine_copy, u, h)
+
         x_codes = keep.tile([P, S], U32, name="x_codes", align_bytes=64)
         x_plane = keep.tile([P, S], U8, name="x_plane", align_bytes=64)
-        for lo in (0, S // 2):
-            hi = lo + S // 2
-            nc.vector.quantize_mx(out=x_codes[:, lo:hi].bitcast(FP8X4), scales=x_plane[:, lo:hi], in_=x_woven[:, PACK * lo : PACK * hi])
+        for h, (lo, hi) in enumerate(halves):
+            nc.vector.quantize_mx(out=x_codes[:, lo:hi].bitcast(FP8X4), scales=x_plane[:, lo:hi], in_=x_woven[h][:])
 
         w1_codes = [keep.tile([P, 2 * P], U32, name="w1_codes%d" % u, align_bytes=64) for u in range(2)]
         w1_plane = [keep.tile([P, 2 * P], U8, name="w1_plane%d" % u, align_bytes=64) for u in range(2)]
         dealt = [keep.tile([P, 2 * P * PACK], BF16, name="w1_dealt%d" % u, align_bytes=64) for u in range(2)]
-        for u, engine_copy in enumerate((nc.vector.tensor_copy, nc.scalar.copy)):
-            engine_copy(
-                out=dealt[u][:].rearrange("p (t m j) -> p m j t", t=2, j=PACK),
-                in_=w1_raw[:].rearrange("p j (m t) -> p m j t", t=PACK)[:, :, :, 2 * u : 2 * u + 2],
+        for u, j0, j1 in ((0, 0, 2), (0, 2, 4), (1, 0, 4)):
+            nc.scalar.copy(
+                out=dealt[u][:].rearrange("p (t m j) -> p m j t", t=2, j=PACK)[:, :, j0:j1, :],
+                in_=w1_raw[:, j0 * H : j1 * H].rearrange("p (j m t) -> p m j t", m=P, t=PACK)[:, :, :, 2 * u : 2 * u + 2],
             )
         for u in range(2):
             nc.vector.quantize_mx(out=w1_codes[u][:].bitcast(FP8X4), scales=w1_plane[u][:], in_=dealt[u][:])
@@ -116,11 +121,12 @@ def tile_picked_posadd_gelu_l_kernel(tc, xT, w1, w2_words, w2_scales, pe, offs, 
                 out=summed[:, t, lo:hi], in0=pe_raw[t][:].indirect(entries(lo, hi)), in1=drained[:, t - 1, lo:hi], op=ADD
             )
 
-        nc.vector.tensor_tensor(out=summed[:, 0, :], in0=first_product(0, 0, S)[:], in1=pe_first[:], op=ADD)
-        for t, lo, hi in ((1, 0, S // 2), (1, S // 2, S), (2, 0, S), (3, 0, S)):
-            nc.scalar.copy(out=drained[:, t - 1, lo:hi], in_=first_product(t, lo, hi)[:])
-            if t < PACK - 1:
-                pick_and_add(t, lo, hi)
+        acc = {t: first_product(t, 0, S) for t in (1, 0, 2, 3)}
+        nc.vector.tensor_tensor(out=summed[:, 0, :], in0=acc[0][:], in1=pe_first[:], op=ADD)
+        for t in range(1, PACK):
+            nc.scalar.copy(out=drained[:, t - 1, :], in_=acc[t][:])
+        for t in (1, 2):
+            pick_and_add(t, 0, S)
 
         pieces = ((0, 2 * CHUNK), (2 * CHUNK, 3 * CHUNK), (3 * CHUNK, S))
         hidden = [keep.tile([P, PACK * (hi - lo)], BF16, name="hidden%d" % lo, align_bytes=64) for lo, hi in pieces]
@@ -153,7 +159,8 @@ def tile_picked_posadd_gelu_l_kernel(tc, xT, w1, w2_words, w2_scales, pe, offs, 
                 stop=True,
             )
             staged = keep.tile([P, hi - lo], F32, name="staged%d" % g)
-            nc.scalar.copy(out=staged[:], in_=result[:])
+            copy_out = nc.scalar.copy if hi == S else nc.vector.tensor_copy
+            copy_out(out=staged[:], in_=result[:])
             nc.sync.dma_start(out=out[:, lo:hi], in_=staged[:])
 
         for g, (lo, hi) in enumerate(pieces):

@@ -19,7 +19,8 @@ ADD = mybir.AluOpType.add
 P = 128
 PACK = 4
 CHUNK = 128
-CHUNKS = S // CHUNK
+LINE = 4
+LAST = 64
 
 
 def tile_picked_posadd_gelu_l_kernel(tc, xT, w1, w2_words, w2_scales, pe, offs, out):
@@ -113,42 +114,47 @@ def tile_picked_posadd_gelu_l_kernel(tc, xT, w1, w2_words, w2_scales, pe, offs, 
             )
             return acc
 
-        summed = keep.tile([P, PACK, S], F32, name="summed")
-        drained = keep.tile([P, PACK - 1, S], F32, name="drained")
+        work = keep.tile([P, PACK, S + 2 * CHUNK], F32, name="work")
+        summed = work[:, :, :S]
+        drained = keep.tile([P, 2, S], F32, name="drained")
+        products = {1: drained[:, 0, :], 2: drained[:, 1, :], 3: work[:, 2, 2 * CHUNK :]}
 
         def pick_and_add(t, lo, hi):
-            nc.vector.tensor_tensor(
-                out=summed[:, t, lo:hi], in0=pe_raw[t][:].indirect(entries(lo, hi)), in1=drained[:, t - 1, lo:hi], op=ADD
-            )
+            nc.vector.tensor_tensor(out=summed[:, t, lo:hi], in0=pe_raw[t][:].indirect(entries(lo, hi)), in1=products[t][:, lo:hi], op=ADD)
 
         acc = {t: first_product(t, 0, S) for t in (1, 0, 2, 3)}
         nc.vector.tensor_tensor(out=summed[:, 0, :], in0=acc[0][:], in1=pe_first[:], op=ADD)
         for t in range(1, PACK):
-            nc.scalar.copy(out=drained[:, t - 1, :], in_=acc[t][:])
-        for t in (1, 2):
-            pick_and_add(t, 0, S)
+            nc.scalar.copy(out=products[t], in_=acc[t][:])
+        pick_and_add(1, 0, S)
+        pick_and_add(2, 0, 2 * CHUNK)
 
-        pieces = ((0, 2 * CHUNK), (2 * CHUNK, 3 * CHUNK), (3 * CHUNK, S))
-        hidden = [keep.tile([P, PACK * (hi - lo)], BF16, name="hidden%d" % lo, align_bytes=64) for lo, hi in pieces]
+        spans = ((0, 2 * CHUNK), (2 * CHUNK, 3 * CHUNK), (3 * CHUNK, S))
+        hidden = [keep.tile([P, PACK * (hi - lo)], BF16, name="hidden%d" % lo, align_bytes=64) for lo, hi in spans]
 
-        def gelu_pair(u, g, lo, hi):
-            at = pieces[g][0]
+        def woven(lo, hi):
+            g = max(lo // CHUNK - 1, 0)
+            return hidden[g][:, PACK * (lo - spans[g][0]) : PACK * (hi - spans[g][0])]
+
+        def gelu_pair(u, lo, hi):
             nc.scalar.activation(
-                out=hidden[g][:, PACK * (lo - at) : PACK * (hi - at)].rearrange("p (s t) -> p s t", t=PACK)[:, :, 2 * u : 2 * u + 2],
+                out=woven(lo, hi).rearrange("p (s t) -> p s t", t=PACK)[:, :, 2 * u : 2 * u + 2],
                 in_=summed[:, 2 * u : 2 * u + 2, lo:hi].rearrange("p t s -> p s t"),
                 func=GELU,
             )
 
-        def first_layer(c, g):
-            pick_and_add(PACK - 1, c * CHUNK, (c + 1) * CHUNK)
-            gelu_pair(1, g, c * CHUNK, (c + 1) * CHUNK)
+        def gelu_whole(lo, hi):
+            nc.scalar.activation(
+                out=woven(lo, hi).rearrange("p (c i t) -> p c t i", i=LINE, t=PACK),
+                in_=summed[:, :, lo:hi].rearrange("p t (c i) -> p c t i", i=LINE),
+                func=GELU,
+            )
 
-        def second_layer(g):
-            lo, hi = pieces[g]
+        def second_layer(g, lo, hi):
             h_codes = keep.tile([P, hi - lo], U32, name="h_codes%d" % g, align_bytes=64)
             h_plane = keep.tile([P, hi - lo], U8, name="h_plane%d" % g, align_bytes=64)
-            nc.vector.quantize_mx(out=h_codes[:].bitcast(FP8X4), scales=h_plane[:], in_=hidden[g][:])
-            result = psum.tile([P, hi - lo], F32, name="result%d" % g)
+            nc.vector.quantize_mx(out=h_codes[:].bitcast(FP8X4), scales=h_plane[:], in_=woven(lo, hi))
+            result = psum.tile([P, hi - lo], F32, name="result%d" % g if g else "acc0_0")
             nc.tensor.matmul_mx(
                 out=result[:],
                 lhsT=w2_codes[:].bitcast(FP8X4),
@@ -158,14 +164,25 @@ def tile_picked_posadd_gelu_l_kernel(tc, xT, w1, w2_words, w2_scales, pe, offs, 
                 start=True,
                 stop=True,
             )
-            staged = keep.tile([P, hi - lo], F32, name="staged%d" % g)
-            copy_out = nc.scalar.copy if hi == S else nc.vector.tensor_copy
-            copy_out(out=staged[:], in_=result[:])
-            nc.sync.dma_start(out=out[:, lo:hi], in_=staged[:])
+            copy_out = nc.vector.tensor_copy if g in (1, 2) else nc.scalar.copy
+            copy_out(out=staged[:, lo:hi], in_=result[:])
 
-        for g, (lo, hi) in enumerate(pieces):
-            gelu_pair(0, g, lo, hi)
-        for c in range(CHUNKS):
-            first_layer(c, max(c - 1, 0))
-        for g in range(len(pieces)):
-            second_layer(g)
+        staged = keep.tile([P, S], F32, name="staged")
+        late = S - CHUNK
+        gelu_pair(0, 0, CHUNK)
+        gelu_pair(0, late, S)
+        pick_and_add(3, 0, CHUNK)
+        gelu_pair(1, 0, CHUNK)
+        pick_and_add(3, CHUNK, 2 * CHUNK)
+        gelu_whole(CHUNK, 2 * CHUNK)
+        pick_and_add(2, 2 * CHUNK, late)
+        pick_and_add(3, 2 * CHUNK, late)
+        gelu_whole(2 * CHUNK, late)
+        pick_and_add(2, late, S)
+        for lo in (late, S - LAST):
+            pick_and_add(3, lo, lo + LAST)
+            gelu_pair(1, lo, lo + LAST)
+        for g, (lo, hi) in enumerate(((0, CHUNK), (CHUNK, 2 * CHUNK), (2 * CHUNK, late), (late, S - LAST), (S - LAST, S))):
+            second_layer(g, lo, hi)
+        for queue, lo, hi in ((nc.sync, 0, CHUNK), (nc.sync, CHUNK, 2 * CHUNK), (nc.sync, 2 * CHUNK, late), (nc.scalar, late, S)):
+            queue.dma_start(out=out[:, lo:hi], in_=staged[:, lo:hi])

@@ -100,11 +100,10 @@ def tile_picked_posadd_gelu_l_kernel(tc, xT, w1, w2_words, w2_scales, pe, offs, 
         pe_first = keep.tile([P, S], F32, name="pe_first")
         nc.vector.tensor_copy(out=pe_first[:], in_=pe_raw[0][:].indirect(offsets[:]))
 
-        def first_product(t, lo, hi):
-            acc = psum.tile([P, hi - lo], F32, name="acc%d_%d" % (t, lo))
+        def first_product(acc, t, lo, hi):
             rows = slice((t % 2) * P, (t % 2 + 1) * P)
             nc.tensor.matmul_mx(
-                out=acc[:],
+                out=acc,
                 lhsT=w1_codes[t // 2][:, rows].bitcast(FP8X4),
                 lhsT_scale=w1_plane[t // 2][:, rows],
                 rhs=x_codes[:, lo:hi].bitcast(FP8X4),
@@ -112,20 +111,25 @@ def tile_picked_posadd_gelu_l_kernel(tc, xT, w1, w2_words, w2_scales, pe, offs, 
                 start=True,
                 stop=True,
             )
-            return acc
 
-        work = keep.tile([P, PACK, S + 2 * CHUNK], F32, name="work")
-        summed = work[:, :, :S]
-        drained = keep.tile([P, 2, S], F32, name="drained")
-        products = {1: drained[:, 0, :], 2: drained[:, 1, :], 3: work[:, 2, 2 * CHUNK :]}
+        work = keep.tile([P, PACK + 1, S + 2 * CHUNK], F32, name="work")
+        summed = work[:, :PACK, :S]
+        drained = keep.tile([P, S], F32, name="drained")
+        products = {1: drained[:], 2: work[:, PACK, 2 * CHUNK :], 3: work[:, 2, 2 * CHUNK :]}
 
         def pick_and_add(t, lo, hi):
             nc.vector.tensor_tensor(out=summed[:, t, lo:hi], in0=pe_raw[t][:].indirect(entries(lo, hi)), in1=products[t][:, lo:hi], op=ADD)
 
-        acc = {t: first_product(t, 0, S) for t in (1, 0, 2, 3)}
+        acc = [psum.tile([P, S], F32, name="acc%d" % t) for t in range(2)]
+        for t in (1, 0):
+            first_product(acc[t][:], t, 0, S)
         nc.vector.tensor_tensor(out=summed[:, 0, :], in0=acc[0][:], in1=pe_first[:], op=ADD)
-        for t in range(1, PACK):
-            nc.scalar.copy(out=products[t], in_=acc[t][:])
+        nc.scalar.copy(out=products[1], in_=acc[1][:])
+        for h, (lo, hi) in enumerate(halves):
+            pair = psum.tile([P, 2, hi - lo], F32, name="pair%d" % h)
+            for e, t in enumerate((3, 2)):
+                first_product(pair[:, e, :], t, lo, hi)
+            nc.scalar.copy(out=work[:, 2::2, 2 * CHUNK + lo : 2 * CHUNK + hi], in_=pair[:])
         pick_and_add(1, 0, S)
         pick_and_add(2, 0, 2 * CHUNK)
 
@@ -154,7 +158,7 @@ def tile_picked_posadd_gelu_l_kernel(tc, xT, w1, w2_words, w2_scales, pe, offs, 
             h_codes = keep.tile([P, hi - lo], U32, name="h_codes%d" % g, align_bytes=64)
             h_plane = keep.tile([P, hi - lo], U8, name="h_plane%d" % g, align_bytes=64)
             nc.vector.quantize_mx(out=h_codes[:].bitcast(FP8X4), scales=h_plane[:], in_=woven(lo, hi))
-            result = psum.tile([P, hi - lo], F32, name="result%d" % g if g else "acc0_0")
+            result = psum.tile([P, hi - lo], F32, name="result%d" % g if g else "acc0")
             nc.tensor.matmul_mx(
                 out=result[:],
                 lhsT=w2_codes[:].bitcast(FP8X4),
@@ -184,5 +188,5 @@ def tile_picked_posadd_gelu_l_kernel(tc, xT, w1, w2_words, w2_scales, pe, offs, 
             gelu_pair(1, lo, lo + LAST)
         for g, (lo, hi) in enumerate(((0, CHUNK), (CHUNK, 2 * CHUNK), (2 * CHUNK, late), (late, S - LAST), (S - LAST, S))):
             second_layer(g, lo, hi)
-        for queue, lo, hi in ((nc.sync, 0, CHUNK), (nc.sync, CHUNK, 2 * CHUNK), (nc.sync, 2 * CHUNK, late), (nc.scalar, late, S)):
+        for queue, lo, hi in ((nc.sync, 0, CHUNK), (nc.sync, CHUNK, 2 * CHUNK), (nc.sync, 2 * CHUNK, late), (nc.sync, late, S)):
             queue.dma_start(out=out[:, lo:hi], in_=staged[:, lo:hi])

@@ -120,16 +120,17 @@ def tile_picked_posadd_gelu_l_kernel(tc, xT, w1, w2_words, w2_scales, pe, offs, 
         def pick_and_add(t, lo, hi):
             nc.vector.tensor_tensor(out=summed[:, t, lo:hi], in0=pe_raw[t][:].indirect(entries(lo, hi)), in1=products[t][:, lo:hi], op=ADD)
 
-        acc = [psum.tile([P, S], F32, name="acc%d" % t) for t in range(2)]
-        for t in (1, 0):
-            first_product(acc[t][:], t, 0, S)
-        nc.vector.tensor_tensor(out=summed[:, 0, :], in0=acc[0][:], in1=pe_first[:], op=ADD)
-        nc.scalar.copy(out=products[1], in_=acc[1][:])
-        for h, (lo, hi) in enumerate(halves):
-            pair = psum.tile([P, 2, hi - lo], F32, name="pair%d" % h)
+        acc = psum.tile([P, S], F32, name="bank0")
+        first_product(acc[:], 1, 0, S)
+        nc.scalar.copy(out=products[1], in_=acc[:])
+        acc = psum.tile([P, S], F32, name="bank1")
+        first_product(acc[:], 0, 0, S)
+        nc.vector.tensor_tensor(out=summed[:, 0, :], in0=acc[:], in1=pe_first[:], op=ADD)
+        for h, (lo, hi) in enumerate(((0, CHUNK), (CHUNK, 2 * CHUNK), (2 * CHUNK, S))):
+            acc = psum.tile([P, 2, hi - lo], F32, name="bank%d" % (2 + h))
             for e, t in enumerate((3, 2)):
-                first_product(pair[:, e, :], t, lo, hi)
-            nc.scalar.copy(out=work[:, 2::2, 2 * CHUNK + lo : 2 * CHUNK + hi], in_=pair[:])
+                first_product(acc[:, e, :], t, lo, hi)
+            nc.scalar.copy(out=work[:, 2::2, 2 * CHUNK + lo : 2 * CHUNK + hi], in_=acc[:])
         pick_and_add(1, 0, S)
         pick_and_add(2, 0, 2 * CHUNK)
 
@@ -145,6 +146,7 @@ def tile_picked_posadd_gelu_l_kernel(tc, xT, w1, w2_words, w2_scales, pe, offs, 
                 out=woven(lo, hi).rearrange("p (s t) -> p s t", t=PACK)[:, :, 2 * u : 2 * u + 2],
                 in_=summed[:, 2 * u : 2 * u + 2, lo:hi].rearrange("p t s -> p s t"),
                 func=GELU,
+                bias=warm_out[:],
             )
 
         def gelu_whole(lo, hi):
@@ -152,13 +154,14 @@ def tile_picked_posadd_gelu_l_kernel(tc, xT, w1, w2_words, w2_scales, pe, offs, 
                 out=woven(lo, hi).rearrange("p (c i t) -> p c t i", i=LINE, t=PACK),
                 in_=summed[:, :, lo:hi].rearrange("p t (c i) -> p c t i", i=LINE),
                 func=GELU,
+                bias=warm_out[:],
             )
 
         def second_layer(g, lo, hi):
             h_codes = keep.tile([P, hi - lo], U32, name="h_codes%d" % g, align_bytes=64)
             h_plane = keep.tile([P, hi - lo], U8, name="h_plane%d" % g, align_bytes=64)
             nc.vector.quantize_mx(out=h_codes[:].bitcast(FP8X4), scales=h_plane[:], in_=woven(lo, hi))
-            result = psum.tile([P, hi - lo], F32, name="result%d" % g if g else "acc0")
+            result = psum.tile([P, hi - lo], F32, name="bank%d" % ((5 + g) % 8))
             nc.tensor.matmul_mx(
                 out=result[:],
                 lhsT=w2_codes[:].bitcast(FP8X4),
@@ -168,7 +171,7 @@ def tile_picked_posadd_gelu_l_kernel(tc, xT, w1, w2_words, w2_scales, pe, offs, 
                 start=True,
                 stop=True,
             )
-            copy_out = nc.vector.tensor_copy if g in (1, 2) else nc.scalar.copy
+            copy_out = nc.vector.tensor_copy if g == 2 else nc.scalar.copy
             copy_out(out=staged[:, lo:hi], in_=result[:])
 
         staged = keep.tile([P, S], F32, name="staged")
@@ -188,5 +191,5 @@ def tile_picked_posadd_gelu_l_kernel(tc, xT, w1, w2_words, w2_scales, pe, offs, 
             gelu_pair(1, lo, lo + LAST)
         for g, (lo, hi) in enumerate(((0, CHUNK), (CHUNK, 2 * CHUNK), (2 * CHUNK, late), (late, S - LAST), (S - LAST, S))):
             second_layer(g, lo, hi)
-        for queue, lo, hi in ((nc.sync, 0, CHUNK), (nc.sync, CHUNK, 2 * CHUNK), (nc.sync, 2 * CHUNK, late), (nc.sync, late, S)):
+        for queue, lo, hi in ((nc.sync, 0, 2 * CHUNK), (nc.sync, 2 * CHUNK, late), (nc.sync, late, S)):
             queue.dma_start(out=out[:, lo:hi], in_=staged[:, lo:hi])

@@ -21,6 +21,7 @@ PACK = 4
 CHUNK = 128
 LINE = 4
 LAST = 64
+SHARE = 40
 
 
 def tile_picked_posadd_gelu_l_kernel(tc, xT, w1, w2_words, w2_scales, pe, offs, out):
@@ -40,10 +41,10 @@ def tile_picked_posadd_gelu_l_kernel(tc, xT, w1, w2_words, w2_scales, pe, offs, 
         w2_codes = keep.tile([P, N], U32, name="w2_codes", align_bytes=64)
         w2_plane = keep.tile([P, N], U8, name="w2_plane", align_bytes=64)
 
-        nc.gpsimd.memset(w2_plane[:].bitcast(I32), 0)
+        nc.vector.memset(w2_plane[:].bitcast(I32), 0)
         warm_in = keep.tile([P, 1], F32, name="warm_in")
         warm_out = keep.tile([P, 1], F32, name="warm_out")
-        nc.gpsimd.memset(warm_in[:], 0.0)
+        nc.vector.memset(warm_in[:], 0.0)
         nc.scalar.activation(out=warm_out[:], in_=warm_in[:], func=GELU)
 
         for j in range(PACK):
@@ -65,21 +66,25 @@ def tile_picked_posadd_gelu_l_kernel(tc, xT, w1, w2_words, w2_scales, pe, offs, 
         halves = ((0, S // 2), (S // 2, S))
         x_woven = [keep.tile([P, PACK * S // 2], BF16, name="x_woven%d" % h, align_bytes=64) for h in range(2)]
 
-        def weave(engine_copy, u, h):
-            lo, hi = halves[h]
+        def weave(engine_copy, u, lo, hi):
+            h = 2 * lo // S
             engine_copy(
-                out=x_woven[h][:].rearrange("p (s j) -> p s j", j=PACK)[:, :, 2 * u : 2 * u + 2],
+                out=x_woven[h][:, PACK * (lo - halves[h][0]) : PACK * (hi - halves[h][0])].rearrange("p (s j) -> p s j", j=PACK)[:, :, 2 * u : 2 * u + 2],
                 in_=x_picked[:, 2 * u : 2 * u + 2, lo:hi].rearrange("p j s -> p s j"),
             )
 
         x_cast = keep.tile([P, T], BF16, name="x_cast")
         nc.scalar.copy(out=x_cast[:], in_=x_raw[0][:])
         nc.scalar.activation(out=x_picked[:, 0, :], in_=x_cast[:].indirect(offsets[:]), func=COPY)
-        for j in range(1, PACK):
+        for j in (1, 2):
             nc.vector.tensor_copy(out=x_picked[:, j, :], in_=x_raw[j][:].indirect(offsets[:]))
-        for u, engine_copy in enumerate((nc.scalar.copy, nc.vector.tensor_copy)):
-            for h in range(2):
-                weave(engine_copy, u, h)
+        for lo, hi in halves:
+            nc.vector.tensor_copy(out=x_picked[:, 3, lo:hi], in_=x_raw[3][:].indirect(entries(lo, hi)))
+        for lo, hi in halves:
+            weave(nc.scalar.copy, 0, lo, hi)
+        weave(nc.scalar.copy, 1, 0, CHUNK)
+        weave(nc.vector.tensor_copy, 1, CHUNK, 2 * CHUNK)
+        weave(nc.vector.tensor_copy, 1, 2 * CHUNK, S)
 
         x_codes = keep.tile([P, S], U32, name="x_codes", align_bytes=64)
         x_plane = keep.tile([P, S], U8, name="x_plane", align_bytes=64)
@@ -89,10 +94,15 @@ def tile_picked_posadd_gelu_l_kernel(tc, xT, w1, w2_words, w2_scales, pe, offs, 
         w1_codes = [keep.tile([P, 2 * P], U32, name="w1_codes%d" % u, align_bytes=64) for u in range(2)]
         w1_plane = [keep.tile([P, 2 * P], U8, name="w1_plane%d" % u, align_bytes=64) for u in range(2)]
         dealt = [keep.tile([P, 2 * P * PACK], BF16, name="w1_dealt%d" % u, align_bytes=64) for u in range(2)]
-        for u, j0, j1 in ((0, 0, 2), (0, 2, 4), (1, 0, 4)):
-            nc.scalar.copy(
-                out=dealt[u][:].rearrange("p (t m j) -> p m j t", t=2, j=PACK)[:, :, j0:j1, :],
-                in_=w1_raw[:, j0 * H : j1 * H].rearrange("p (j m t) -> p m j t", m=P, t=PACK)[:, :, :, 2 * u : 2 * u + 2],
+        for engine_copy, u, j0, j1, m0, m1 in (
+            (nc.scalar.copy, 0, 0, 2, 0, P),
+            (nc.scalar.copy, 0, 2, 4, 0, P - SHARE),
+            (nc.vector.tensor_copy, 0, 2, 4, P - SHARE, P),
+            (nc.scalar.copy, 1, 0, 4, 0, P),
+        ):
+            engine_copy(
+                out=dealt[u][:].rearrange("p (t m j) -> p m j t", t=2, j=PACK)[:, m0:m1, j0:j1, :],
+                in_=w1_raw[:, j0 * H : j1 * H].rearrange("p (j m t) -> p m j t", m=P, t=PACK)[:, m0:m1, :, 2 * u : 2 * u + 2],
             )
         for u in range(2):
             nc.vector.quantize_mx(out=w1_codes[u][:].bitcast(FP8X4), scales=w1_plane[u][:], in_=dealt[u][:])

@@ -22,6 +22,7 @@ CHUNK = 128
 LINE = 4
 LAST = 64
 SHARE = 40
+SHARE_LATE = 32
 
 
 def tile_picked_posadd_gelu_l_kernel(tc, xT, w1, w2_words, w2_scales, pe, offs, out):
@@ -98,7 +99,8 @@ def tile_picked_posadd_gelu_l_kernel(tc, xT, w1, w2_words, w2_scales, pe, offs, 
             (nc.scalar.copy, 0, 0, 2, 0, P),
             (nc.scalar.copy, 0, 2, 4, 0, P - SHARE),
             (nc.vector.tensor_copy, 0, 2, 4, P - SHARE, P),
-            (nc.scalar.copy, 1, 0, 4, 0, P),
+            (nc.scalar.copy, 1, 0, 4, 0, P - SHARE_LATE),
+            (nc.vector.tensor_copy, 1, 0, 4, P - SHARE_LATE, P),
         ):
             engine_copy(
                 out=dealt[u][:].rearrange("p (t m j) -> p m j t", t=2, j=PACK)[:, m0:m1, j0:j1, :],
@@ -107,8 +109,8 @@ def tile_picked_posadd_gelu_l_kernel(tc, xT, w1, w2_words, w2_scales, pe, offs, 
         for u in range(2):
             nc.vector.quantize_mx(out=w1_codes[u][:].bitcast(FP8X4), scales=w1_plane[u][:], in_=dealt[u][:])
 
-        pe_first = keep.tile([P, S], F32, name="pe_first")
-        nc.vector.tensor_copy(out=pe_first[:], in_=pe_raw[0][:].indirect(offsets[:]))
+        pe_first = keep.tile([P, S // 2], F32, name="pe_first")
+        nc.vector.tensor_copy(out=pe_first[:], in_=pe_raw[0][:].indirect(entries(0, S // 2)))
 
         def first_product(acc, t, lo, hi):
             rows = slice((t % 2) * P, (t % 2 + 1) * P)
@@ -124,24 +126,29 @@ def tile_picked_posadd_gelu_l_kernel(tc, xT, w1, w2_words, w2_scales, pe, offs, 
 
         work = keep.tile([P, PACK + 1, S + 2 * CHUNK], F32, name="work")
         summed = work[:, :PACK, :S]
-        drained = keep.tile([P, S], F32, name="drained")
-        products = {1: drained[:], 2: work[:, PACK, 2 * CHUNK :], 3: work[:, 2, 2 * CHUNK :]}
+        drained = keep.tile([P, 2, S], F32, name="drained")
+        products = {0: drained[:, 0, :], 1: drained[:, 1, :], 2: work[:, PACK, 2 * CHUNK :], 3: work[:, 2, 2 * CHUNK :]}
 
         def pick_and_add(t, lo, hi):
             nc.vector.tensor_tensor(out=summed[:, t, lo:hi], in0=pe_raw[t][:].indirect(entries(lo, hi)), in1=products[t][:, lo:hi], op=ADD)
 
-        acc = psum.tile([P, S], F32, name="bank0")
-        first_product(acc[:], 1, 0, S)
-        nc.scalar.copy(out=products[1], in_=acc[:])
-        acc = psum.tile([P, S], F32, name="bank1")
-        first_product(acc[:], 0, 0, S)
-        nc.vector.tensor_tensor(out=summed[:, 0, :], in0=acc[:], in1=pe_first[:], op=ADD)
+        acc = psum.tile([P, S // 2], F32, name="bank1")
+        first_product(acc[:], 0, S // 2, S)
+        nc.scalar.copy(out=products[0][:, S // 2 :], in_=acc[:])
+        acc = psum.tile([P, S // 2], F32, name="bank7")
+        first_product(acc[:], 0, 0, S // 2)
+        nc.vector.tensor_tensor(out=summed[:, 0, : S // 2], in0=acc[:], in1=pe_first[:], op=ADD)
+        pick_and_add(0, S // 2, S)
+        for bank, (lo, hi) in zip((0, 6), halves):
+            acc = psum.tile([P, S // 2], F32, name="bank%d" % bank)
+            first_product(acc[:], 1, lo, hi)
+            nc.scalar.copy(out=products[1][:, lo:hi], in_=acc[:])
+            pick_and_add(1, lo, hi)
         for h, (lo, hi) in enumerate(((0, CHUNK), (CHUNK, 2 * CHUNK), (2 * CHUNK, S))):
             acc = psum.tile([P, 2, hi - lo], F32, name="bank%d" % (2 + h))
             for e, t in enumerate((3, 2)):
                 first_product(acc[:, e, :], t, lo, hi)
             nc.scalar.copy(out=work[:, 2::2, 2 * CHUNK + lo : 2 * CHUNK + hi], in_=acc[:])
-        pick_and_add(1, 0, S)
         pick_and_add(2, 0, 2 * CHUNK)
 
         spans = ((0, 2 * CHUNK), (2 * CHUNK, 3 * CHUNK), (3 * CHUNK, S))

@@ -151,12 +151,11 @@ def tile_picked_posadd_gelu_l_kernel(tc, xT, w1, w2_words, w2_scales, pe, offs, 
             nc.scalar.copy(out=work[:, 2::2, 2 * CHUNK + lo : 2 * CHUNK + hi], in_=acc[:])
         pick_and_add(2, 0, 2 * CHUNK)
 
-        spans = ((0, 2 * CHUNK), (2 * CHUNK, 3 * CHUNK), (3 * CHUNK, S))
-        hidden = [keep.tile([P, PACK * (hi - lo)], BF16, name="hidden%d" % lo, align_bytes=64) for lo, hi in spans]
+        hidden = [keep.tile([P, PACK * (hi - lo)], BF16, name="hidden%d" % lo, align_bytes=64) for lo, hi in halves]
 
         def woven(lo, hi):
-            g = max(lo // CHUNK - 1, 0)
-            return hidden[g][:, PACK * (lo - spans[g][0]) : PACK * (hi - spans[g][0])]
+            g = 2 * lo // S
+            return hidden[g][:, PACK * (lo - halves[g][0]) : PACK * (hi - halves[g][0])]
 
         def gelu_pair(u, lo, hi):
             nc.scalar.activation(
@@ -194,14 +193,14 @@ def tile_picked_posadd_gelu_l_kernel(tc, xT, w1, w2_words, w2_scales, pe, offs, 
         staged = keep.tile([P, S], F32, name="staged")
         late = S - CHUNK
         gelu_pair(0, 0, CHUNK)
-        gelu_pair(0, late, S)
+        gelu_pair(0, 2 * CHUNK, S)
         pick_and_add(3, 0, CHUNK)
         gelu_pair(1, 0, CHUNK)
         pick_and_add(3, CHUNK, 2 * CHUNK)
         gelu_whole(CHUNK, 2 * CHUNK)
         pick_and_add(2, 2 * CHUNK, late)
         pick_and_add(3, 2 * CHUNK, late)
-        gelu_whole(2 * CHUNK, late)
+        gelu_pair(1, 2 * CHUNK, late)
         pick_and_add(2, late, S)
         for lo in (late, S - LAST):
             pick_and_add(3, lo, lo + LAST)

@@ -22,7 +22,7 @@ CHUNK = 128
 LINE = 4
 LAST = 64
 SHARE = 40
-SHARE_LATE = 32
+SHARE_LATE = 48
 
 
 def tile_picked_posadd_gelu_l_kernel(tc, xT, w1, w2_words, w2_scales, pe, offs, out):

@@ -19,10 +19,11 @@ ADD = mybir.AluOpType.add
 P = 128
 PACK = 4
 CHUNK = 128
+HALF = S // 2
 LINE = 4
 LAST = 64
-SHARE = 40
-SHARE_LATE = 48
+FIRST_SHARE = 82
+SECOND_SHARE = 76
 
 
 def tile_picked_posadd_gelu_l_kernel(tc, xT, w1, w2_words, w2_scales, pe, offs, out):
@@ -52,8 +53,7 @@ def tile_picked_posadd_gelu_l_kernel(tc, xT, w1, w2_words, w2_scales, pe, offs, 
             nc.sync.dma_start(out=x_raw[j][:], in_=x_rows[:, j, :])
             if j == 0:
                 nc.sync.dma_start(offsets[:], offs)
-        for u in range(2):
-            nc.sync.dma_start(out=w1_raw[:, 2 * u * H : 2 * (u + 1) * H], in_=w1_rows[:, 2 * u * H : 2 * (u + 1) * H])
+        nc.sync.dma_start(out=w1_raw[:], in_=w1_rows)
         for t in range(PACK):
             nc.sync.dma_start(out=pe_raw[t][:], in_=pe_rows[:, t, :])
         nc.sync.dma_start(out=w2_codes[:].bitcast(I32), in_=w2_words[0].rearrange("p n r -> p (n r)").bitcast(I32))
@@ -63,59 +63,57 @@ def tile_picked_posadd_gelu_l_kernel(tc, xT, w1, w2_words, w2_scales, pe, offs, 
         def entries(lo, hi):
             return offsets[:, lo // 16 : hi // 16]
 
-        x_picked = keep.tile([P, PACK, S], BF16, name="x_picked")
-        halves = ((0, S // 2), (S // 2, S))
-        x_woven = [keep.tile([P, PACK * S // 2], BF16, name="x_woven%d" % h, align_bytes=64) for h in range(2)]
+        def scalar_pick(out, in_):
+            nc.scalar.activation(out=out, in_=in_, func=COPY)
 
-        def weave(engine_copy, u, lo, hi):
-            h = 2 * lo // S
+        def words(tiles, lo, hi):
+            g = lo // HALF
+            return tiles[g][:, PACK * (lo - g * HALF) : PACK * (hi - g * HALF)]
+
+        x_picked = keep.tile([P, PACK, S], BF16, name="x_picked")
+        x_woven = [keep.tile([P, PACK * HALF], BF16, name="x_woven%d" % g, align_bytes=64) for g in range(2)]
+
+        def pick_x(pick, j, lo, hi):
+            pick(out=x_picked[:, j, lo:hi], in_=x_raw[j][:].indirect(entries(lo, hi)))
+
+        def weave(engine_copy, lo, hi):
             engine_copy(
-                out=x_woven[h][:, PACK * (lo - halves[h][0]) : PACK * (hi - halves[h][0])].rearrange("p (s j) -> p s j", j=PACK)[:, :, 2 * u : 2 * u + 2],
-                in_=x_picked[:, 2 * u : 2 * u + 2, lo:hi].rearrange("p j s -> p s j"),
+                out=words(x_woven, lo, hi).rearrange("p (c i j) -> p c j i", i=LINE, j=PACK),
+                in_=x_picked[:, :, lo:hi].rearrange("p j (c i) -> p c j i", i=LINE),
             )
 
-        x_cast = keep.tile([P, T], BF16, name="x_cast")
-        nc.scalar.copy(out=x_cast[:], in_=x_raw[0][:])
-        nc.scalar.activation(out=x_picked[:, 0, :], in_=x_cast[:].indirect(offsets[:]), func=COPY)
-        for j in (1, 2):
-            nc.vector.tensor_copy(out=x_picked[:, j, :], in_=x_raw[j][:].indirect(offsets[:]))
-        for lo, hi in halves:
-            nc.vector.tensor_copy(out=x_picked[:, 3, lo:hi], in_=x_raw[3][:].indirect(entries(lo, hi)))
-        for lo, hi in halves:
-            weave(nc.scalar.copy, 0, lo, hi)
-        weave(nc.scalar.copy, 1, 0, CHUNK)
-        weave(nc.vector.tensor_copy, 1, CHUNK, 2 * CHUNK)
-        weave(nc.vector.tensor_copy, 1, 2 * CHUNK, S)
+        pick_x(nc.vector.tensor_copy, 0, 0, S)
+        pick_x(scalar_pick, 1, 0, S)
+        pick_x(nc.vector.tensor_copy, 2, 0, S)
+        pick_x(nc.vector.tensor_copy, 3, S - CHUNK, S)
+        for lo in range(0, S - CHUNK, CHUNK):
+            pick_x(scalar_pick, 3, lo, lo + CHUNK)
+            weave(nc.vector.tensor_copy, lo, lo + CHUNK)
+        weave(nc.scalar.copy, S - CHUNK, S)
 
         x_codes = keep.tile([P, S], U32, name="x_codes", align_bytes=64)
         x_plane = keep.tile([P, S], U8, name="x_plane", align_bytes=64)
-        for h, (lo, hi) in enumerate(halves):
-            nc.vector.quantize_mx(out=x_codes[:, lo:hi].bitcast(FP8X4), scales=x_plane[:, lo:hi], in_=x_woven[h][:])
+        for g in range(2):
+            cols = slice(g * HALF, (g + 1) * HALF)
+            nc.vector.quantize_mx(out=x_codes[:, cols].bitcast(FP8X4), scales=x_plane[:, cols], in_=x_woven[g][:])
 
         w1_codes = [keep.tile([P, 2 * P], U32, name="w1_codes%d" % u, align_bytes=64) for u in range(2)]
         w1_plane = [keep.tile([P, 2 * P], U8, name="w1_plane%d" % u, align_bytes=64) for u in range(2)]
         dealt = [keep.tile([P, 2 * P * PACK], BF16, name="w1_dealt%d" % u, align_bytes=64) for u in range(2)]
-        for engine_copy, u, j0, j1, m0, m1 in (
-            (nc.scalar.copy, 0, 0, 2, 0, P),
-            (nc.scalar.copy, 0, 2, 4, 0, P - SHARE),
-            (nc.vector.tensor_copy, 0, 2, 4, P - SHARE, P),
-            (nc.scalar.copy, 1, 0, 4, 0, P - SHARE_LATE),
-            (nc.vector.tensor_copy, 1, 0, 4, P - SHARE_LATE, P),
-        ):
-            engine_copy(
-                out=dealt[u][:].rearrange("p (t m j) -> p m j t", t=2, j=PACK)[:, m0:m1, j0:j1, :],
-                in_=w1_raw[:, j0 * H : j1 * H].rearrange("p (j m t) -> p m j t", m=P, t=PACK)[:, m0:m1, :, 2 * u : 2 * u + 2],
-            )
+        for u, share in enumerate((FIRST_SHARE, SECOND_SHARE)):
+            for engine_copy, m0, m1 in ((nc.vector.tensor_copy, 0, share), (nc.scalar.copy, share, P)):
+                engine_copy(
+                    out=dealt[u][:].rearrange("p (t m j) -> p m j t", t=2, j=PACK)[:, m0:m1, :, :],
+                    in_=w1_raw[:].rearrange("p (j m t) -> p m j t", m=P, t=PACK)[:, m0:m1, :, 2 * u : 2 * u + 2],
+                )
         for u in range(2):
             nc.vector.quantize_mx(out=w1_codes[u][:].bitcast(FP8X4), scales=w1_plane[u][:], in_=dealt[u][:])
 
-        pe_first = keep.tile([P, S // 2], F32, name="pe_first")
-        nc.vector.tensor_copy(out=pe_first[:], in_=pe_raw[0][:].indirect(entries(0, S // 2)))
-
-        def first_product(acc, t, lo, hi):
+        def first_product(bank, t, lo, hi):
+            acc = psum.tile([P, hi - lo], F32, name="bank%d" % bank)
             rows = slice((t % 2) * P, (t % 2 + 1) * P)
             nc.tensor.matmul_mx(
-                out=acc,
+                out=acc[:],
                 lhsT=w1_codes[t // 2][:, rows].bitcast(FP8X4),
                 lhsT_scale=w1_plane[t // 2][:, rows],
                 rhs=x_codes[:, lo:hi].bitcast(FP8X4),
@@ -123,43 +121,37 @@ def tile_picked_posadd_gelu_l_kernel(tc, xT, w1, w2_words, w2_scales, pe, offs, 
                 start=True,
                 stop=True,
             )
+            return acc
 
-        work = keep.tile([P, PACK + 1, S + 2 * CHUNK], F32, name="work")
+        late = S - CHUNK
+        pe_first = keep.tile([P, S], F32, name="pe_first")
+        for lo, hi in ((0, HALF), (HALF, late)):
+            scalar_pick(out=pe_first[:, lo:hi], in_=pe_raw[0][:].indirect(entries(lo, hi)))
+        nc.vector.tensor_copy(out=pe_first[:, late:], in_=pe_raw[0][:].indirect(entries(late, S)))
+
+        work = keep.tile([P, PACK + 2, late + S], F32, name="pe_raw0")
         summed = work[:, :PACK, :S]
-        drained = keep.tile([P, 2, S], F32, name="drained")
-        products = {0: drained[:, 0, :], 1: drained[:, 1, :], 2: work[:, PACK, 2 * CHUNK :], 3: work[:, 2, 2 * CHUNK :]}
+        side = {1: work[:, PACK, :S], 2: work[:, PACK + 1, :S], 3: work[:, 2, late:]}
 
         def pick_and_add(t, lo, hi):
-            nc.vector.tensor_tensor(out=summed[:, t, lo:hi], in0=pe_raw[t][:].indirect(entries(lo, hi)), in1=products[t][:, lo:hi], op=ADD)
+            nc.vector.tensor_tensor(out=summed[:, t, lo:hi], in0=pe_raw[t][:].indirect(entries(lo, hi)), in1=side[t][:, lo:hi], op=ADD)
 
-        acc = psum.tile([P, S // 2], F32, name="bank1")
-        first_product(acc[:], 0, S // 2, S)
-        nc.scalar.copy(out=products[0][:, S // 2 :], in_=acc[:])
-        acc = psum.tile([P, S // 2], F32, name="bank7")
-        first_product(acc[:], 0, 0, S // 2)
-        nc.vector.tensor_tensor(out=summed[:, 0, : S // 2], in0=acc[:], in1=pe_first[:], op=ADD)
-        pick_and_add(0, S // 2, S)
-        for bank, (lo, hi) in zip((0, 6), halves):
-            acc = psum.tile([P, S // 2], F32, name="bank%d" % bank)
-            first_product(acc[:], 1, lo, hi)
-            nc.scalar.copy(out=products[1][:, lo:hi], in_=acc[:])
+        for g in range(2):
+            lo, hi = g * HALF, (g + 1) * HALF
+            acc0 = first_product(2 * g, 0, lo, hi)
+            acc1 = first_product(2 * g + 1, 1, lo, hi)
+            nc.vector.tensor_tensor(out=summed[:, 0, lo:hi], in0=acc0[:], in1=pe_first[:, lo:hi], op=ADD)
+            nc.scalar.copy(out=side[1][:, lo:hi], in_=acc1[:])
             pick_and_add(1, lo, hi)
-        for h, (lo, hi) in enumerate(((0, CHUNK), (CHUNK, 2 * CHUNK), (2 * CHUNK, S))):
-            acc = psum.tile([P, 2, hi - lo], F32, name="bank%d" % (2 + h))
-            for e, t in enumerate((3, 2)):
-                first_product(acc[:, e, :], t, lo, hi)
-            nc.scalar.copy(out=work[:, 2::2, 2 * CHUNK + lo : 2 * CHUNK + hi], in_=acc[:])
-        pick_and_add(2, 0, 2 * CHUNK)
+        for t in (2, 3):
+            acc = first_product(2 + t, t, 0, S)
+            nc.scalar.copy(out=side[t], in_=acc[:])
 
-        hidden = [keep.tile([P, PACK * (hi - lo)], BF16, name="hidden%d" % lo, align_bytes=64) for lo, hi in halves]
-
-        def woven(lo, hi):
-            g = 2 * lo // S
-            return hidden[g][:, PACK * (lo - halves[g][0]) : PACK * (hi - halves[g][0])]
+        hidden = [keep.tile([P, PACK * HALF], BF16, name="hidden%d" % g, align_bytes=64) for g in range(2)]
 
         def gelu_pair(u, lo, hi):
             nc.scalar.activation(
-                out=woven(lo, hi).rearrange("p (s t) -> p s t", t=PACK)[:, :, 2 * u : 2 * u + 2],
+                out=words(hidden, lo, hi).rearrange("p (s t) -> p s t", t=PACK)[:, :, 2 * u : 2 * u + 2],
                 in_=summed[:, 2 * u : 2 * u + 2, lo:hi].rearrange("p t s -> p s t"),
                 func=GELU,
                 bias=warm_out[:],
@@ -167,17 +159,19 @@ def tile_picked_posadd_gelu_l_kernel(tc, xT, w1, w2_words, w2_scales, pe, offs, 
 
         def gelu_whole(lo, hi):
             nc.scalar.activation(
-                out=woven(lo, hi).rearrange("p (c i t) -> p c t i", i=LINE, t=PACK),
+                out=words(hidden, lo, hi).rearrange("p (c i t) -> p c t i", i=LINE, t=PACK),
                 in_=summed[:, :, lo:hi].rearrange("p t (c i) -> p c t i", i=LINE),
                 func=GELU,
                 bias=warm_out[:],
             )
 
+        staged = keep.tile([P, S], F32, name="staged")
+
         def second_layer(g, lo, hi):
             h_codes = keep.tile([P, hi - lo], U32, name="h_codes%d" % g, align_bytes=64)
             h_plane = keep.tile([P, hi - lo], U8, name="h_plane%d" % g, align_bytes=64)
-            nc.vector.quantize_mx(out=h_codes[:].bitcast(FP8X4), scales=h_plane[:], in_=woven(lo, hi))
-            result = psum.tile([P, hi - lo], F32, name="bank%d" % ((5 + g) % 8))
+            nc.vector.quantize_mx(out=h_codes[:].bitcast(FP8X4), scales=h_plane[:], in_=words(hidden, lo, hi))
+            result = psum.tile([P, hi - lo], F32, name="bank%d" % ((6 + g) % 8))
             nc.tensor.matmul_mx(
                 out=result[:],
                 lhsT=w2_codes[:].bitcast(FP8X4),
@@ -190,22 +184,19 @@ def tile_picked_posadd_gelu_l_kernel(tc, xT, w1, w2_words, w2_scales, pe, offs, 
             copy_out = nc.vector.tensor_copy if g == 2 else nc.scalar.copy
             copy_out(out=staged[:, lo:hi], in_=result[:])
 
-        staged = keep.tile([P, S], F32, name="staged")
-        late = S - CHUNK
-        gelu_pair(0, 0, CHUNK)
-        gelu_pair(0, 2 * CHUNK, S)
+        pick_and_add(2, 0, late)
+        gelu_pair(0, CHUNK, HALF)
+        gelu_pair(0, HALF, S)
         pick_and_add(3, 0, CHUNK)
-        gelu_pair(1, 0, CHUNK)
-        pick_and_add(3, CHUNK, 2 * CHUNK)
-        gelu_whole(CHUNK, 2 * CHUNK)
-        pick_and_add(2, 2 * CHUNK, late)
-        pick_and_add(3, 2 * CHUNK, late)
-        gelu_pair(1, 2 * CHUNK, late)
+        gelu_whole(0, CHUNK)
+        for lo in (CHUNK, HALF):
+            pick_and_add(3, lo, lo + CHUNK)
+            gelu_pair(1, lo, lo + CHUNK)
         pick_and_add(2, late, S)
         for lo in (late, S - LAST):
             pick_and_add(3, lo, lo + LAST)
             gelu_pair(1, lo, lo + LAST)
-        for g, (lo, hi) in enumerate(((0, CHUNK), (CHUNK, 2 * CHUNK), (2 * CHUNK, late), (late, S - LAST), (S - LAST, S))):
+        for g, (lo, hi) in enumerate(((0, CHUNK), (CHUNK, HALF), (HALF, late), (late, S - LAST), (S - LAST, S))):
             second_layer(g, lo, hi)
-        for queue, lo, hi in ((nc.sync, 0, 2 * CHUNK), (nc.sync, 2 * CHUNK, late), (nc.sync, late, S)):
-            queue.dma_start(out=out[:, lo:hi], in_=staged[:, lo:hi])
+        for lo, hi in ((0, HALF), (HALF, late), (late, S)):
+            nc.sync.dma_start(out=out[:, lo:hi], in_=staged[:, lo:hi])

@@ -20,7 +20,7 @@ P = 128
 PACK = 4
 CHUNK = 128
 HALF = S // 2
-LINE = 4
+LINE = 2
 LAST = 64
 FIRST_SHARE = 82
 SECOND_SHARE = 76
@@ -70,7 +70,7 @@ def tile_picked_posadd_gelu_l_kernel(tc, xT, w1, w2_words, w2_scales, pe, offs, 
             g = lo // HALF
             return tiles[g][:, PACK * (lo - g * HALF) : PACK * (hi - g * HALF)]
 
-        x_picked = keep.tile([P, PACK, S], BF16, name="x_picked")
+        x_picked = keep.tile([P, PACK, S], F32, name="x_picked")
         x_woven = [keep.tile([P, PACK * HALF], BF16, name="x_woven%d" % g, align_bytes=64) for g in range(2)]
 
         def pick_x(pick, j, lo, hi):

from contextlib import ExitStack

import concourse.mybir as mybir

K, T, S, H, N = 512, 1024, 512, 512, 128
FLOPS = 2 * K * H * S + 2 * H * N * S

F32 = mybir.dt.float32
BF16 = mybir.dt.bfloat16
I32 = mybir.dt.int32
U32 = mybir.dt.uint32
U16 = mybir.dt.uint16
U8 = mybir.dt.uint8
FP8X4 = mybir.dt.float8_e4m3fn_x4
GELU = mybir.ActivationFunctionType.Gelu_apprx_tanh
COPY = mybir.ActivationFunctionType.Copy
ADD = mybir.AluOpType.add

P = 128
PACK = 4
CHUNK = 128
HALF = S // 2
LINE = 2
LAST = 64
FIRST_SHARE = 82
SECOND_SHARE = 76


def tile_picked_posadd_gelu_l_kernel(tc, xT, w1, w2_words, w2_scales, pe, offs, out):
    nc = tc.nc
    with ExitStack() as ctx:
        keep = ctx.enter_context(tc.tile_pool(name="keep", bufs=1))
        psum = ctx.enter_context(tc.psum_pool(name="psum", bufs=1))

        x_rows = xT.rearrange("(p j) c -> p j c", j=PACK)
        w1_rows = w1.rearrange("(p j) c -> p (j c)", j=PACK)
        pe_rows = pe.rearrange("(p t) c -> p t c", t=PACK)

        offsets = keep.tile([P, S // 16], U16, name="offsets")
        x_raw = [keep.tile([P, T], F32, name="x_raw%d" % j) for j in range(PACK)]
        w1_raw = keep.tile([P, PACK * H], F32, name="w1_raw")
        pe_raw = [keep.tile([P, T], F32, name="pe_raw%d" % t) for t in range(PACK)]
        w2_codes = keep.tile([P, N], U32, name="w2_codes", align_bytes=64)
        w2_plane = keep.tile([P, N], U8, name="w2_plane", align_bytes=64)

        nc.vector.memset(w2_plane[:].bitcast(I32), 0)
        warm_in = keep.tile([P, 1], F32, name="warm_in")
        warm_out = keep.tile([P, 1], F32, name="warm_out")
        nc.vector.memset(warm_in[:], 0.0)
        nc.scalar.activation(out=warm_out[:], in_=warm_in[:], func=GELU)

        for j in range(PACK):
            nc.sync.dma_start(out=x_raw[j][:], in_=x_rows[:, j, :])
            if j == 0:
                nc.sync.dma_start(offsets[:], offs)
        nc.sync.dma_start(out=w1_raw[:], in_=w1_rows)
        for t in range(PACK):
            nc.sync.dma_start(out=pe_raw[t][:], in_=pe_rows[:, t, :])
        nc.sync.dma_start(out=w2_codes[:].bitcast(I32), in_=w2_words[0].rearrange("p n r -> p (n r)").bitcast(I32))
        for q in range(4):
            nc.sync.dma_start(out=w2_plane[32 * q : 32 * q + 4, :].bitcast(I32), in_=w2_scales[0, 4 * q : 4 * q + 4, :].bitcast(I32))

        def entries(lo, hi):
            return offsets[:, lo // 16 : hi // 16]

        def scalar_pick(out, in_):
            nc.scalar.activation(out=out, in_=in_, func=COPY)

        def words(tiles, lo, hi):
            g = lo // HALF
            return tiles[g][:, PACK * (lo - g * HALF) : PACK * (hi - g * HALF)]

        x_picked = keep.tile([P, PACK, S], F32, name="x_picked")
        x_woven = [keep.tile([P, PACK * HALF], BF16, name="x_woven%d" % g, align_bytes=64) for g in range(2)]

        def pick_x(pick, j, lo, hi):
            pick(out=x_picked[:, j, lo:hi], in_=x_raw[j][:].indirect(entries(lo, hi)))

        def weave(engine_copy, lo, hi):
            engine_copy(
                out=words(x_woven, lo, hi).rearrange("p (c i j) -> p c j i", i=LINE, j=PACK),
                in_=x_picked[:, :, lo:hi].rearrange("p j (c i) -> p c j i", i=LINE),
            )

        pick_x(nc.vector.tensor_copy, 0, 0, S)
        pick_x(scalar_pick, 1, 0, S)
        pick_x(nc.vector.tensor_copy, 2, 0, S)
        pick_x(nc.vector.tensor_copy, 3, S - CHUNK, S)
        for lo in range(0, S - CHUNK, CHUNK):
            pick_x(scalar_pick, 3, lo, lo + CHUNK)
            weave(nc.vector.tensor_copy, lo, lo + CHUNK)
        weave(nc.scalar.copy, S - CHUNK, S)

        x_codes = keep.tile([P, S], U32, name="x_codes", align_bytes=64)
        x_plane = keep.tile([P, S], U8, name="x_plane", align_bytes=64)
        for g in range(2):
            cols = slice(g * HALF, (g + 1) * HALF)
            nc.vector.quantize_mx(out=x_codes[:, cols].bitcast(FP8X4), scales=x_plane[:, cols], in_=x_woven[g][:])

        w1_codes = [keep.tile([P, 2 * P], U32, name="w1_codes%d" % u, align_bytes=64) for u in range(2)]
        w1_plane = [keep.tile([P, 2 * P], U8, name="w1_plane%d" % u, align_bytes=64) for u in range(2)]
        dealt = [keep.tile([P, 2 * P * PACK], BF16, name="w1_dealt%d" % u, align_bytes=64) for u in range(2)]
        for u, share in enumerate((FIRST_SHARE, SECOND_SHARE)):
            for engine_copy, m0, m1 in ((nc.vector.tensor_copy, 0, share), (nc.scalar.copy, share, P)):
                engine_copy(
                    out=dealt[u][:].rearrange("p (t m j) -> p m j t", t=2, j=PACK)[:, m0:m1, :, :],
                    in_=w1_raw[:].rearrange("p (j m t) -> p m j t", m=P, t=PACK)[:, m0:m1, :, 2 * u : 2 * u + 2],
                )
        for u in range(2):
            nc.vector.quantize_mx(out=w1_codes[u][:].bitcast(FP8X4), scales=w1_plane[u][:], in_=dealt[u][:])

        def first_product(bank, t, lo, hi):
            acc = psum.tile([P, hi - lo], F32, name="bank%d" % bank)
            rows = slice((t % 2) * P, (t % 2 + 1) * P)
            nc.tensor.matmul_mx(
                out=acc[:],
                lhsT=w1_codes[t // 2][:, rows].bitcast(FP8X4),
                lhsT_scale=w1_plane[t // 2][:, rows],
                rhs=x_codes[:, lo:hi].bitcast(FP8X4),
                rhs_scale=x_plane[:, lo:hi],
                start=True,
                stop=True,
            )
            return acc

        late = S - CHUNK
        pe_first = keep.tile([P, S], F32, name="pe_first")
        for lo, hi in ((0, HALF), (HALF, late)):
            scalar_pick(out=pe_first[:, lo:hi], in_=pe_raw[0][:].indirect(entries(lo, hi)))
        nc.vector.tensor_copy(out=pe_first[:, late:], in_=pe_raw[0][:].indirect(entries(late, S)))

        work = keep.tile([P, PACK + 2, late + S], F32, name="pe_raw0")
        summed = work[:, :PACK, :S]
        side = {1: work[:, PACK, :S], 2: work[:, PACK + 1, :S], 3: work[:, 2, late:]}

        def pick_and_add(t, lo, hi):
            nc.vector.tensor_tensor(out=summed[:, t, lo:hi], in0=pe_raw[t][:].indirect(entries(lo, hi)), in1=side[t][:, lo:hi], op=ADD)

        for g in range(2):
            lo, hi = g * HALF, (g + 1) * HALF
            acc0 = first_product(2 * g, 0, lo, hi)
            acc1 = first_product(2 * g + 1, 1, lo, hi)
            nc.vector.tensor_tensor(out=summed[:, 0, lo:hi], in0=acc0[:], in1=pe_first[:, lo:hi], op=ADD)
            nc.scalar.copy(out=side[1][:, lo:hi], in_=acc1[:])
            pick_and_add(1, lo, hi)
        for t in (2, 3):
            acc = first_product(2 + t, t, 0, S)
            nc.scalar.copy(out=side[t], in_=acc[:])

        hidden = [keep.tile([P, PACK * HALF], BF16, name="hidden%d" % g, align_bytes=64) for g in range(2)]

        def gelu_pair(u, lo, hi):
            nc.scalar.activation(
                out=words(hidden, lo, hi).rearrange("p (s t) -> p s t", t=PACK)[:, :, 2 * u : 2 * u + 2],
                in_=summed[:, 2 * u : 2 * u + 2, lo:hi].rearrange("p t s -> p s t"),
                func=GELU,
                bias=warm_out[:],
            )

        def gelu_whole(lo, hi):
            nc.scalar.activation(
                out=words(hidden, lo, hi).rearrange("p (c i t) -> p c t i", i=LINE, t=PACK),
                in_=summed[:, :, lo:hi].rearrange("p t (c i) -> p c t i", i=LINE),
                func=GELU,
                bias=warm_out[:],
            )

        staged = keep.tile([P, S], F32, name="staged")

        def second_layer(g, lo, hi):
            h_codes = keep.tile([P, hi - lo], U32, name="h_codes%d" % g, align_bytes=64)
            h_plane = keep.tile([P, hi - lo], U8, name="h_plane%d" % g, align_bytes=64)
            nc.vector.quantize_mx(out=h_codes[:].bitcast(FP8X4), scales=h_plane[:], in_=words(hidden, lo, hi))
            result = psum.tile([P, hi - lo], F32, name="bank%d" % ((6 + g) % 8))
            nc.tensor.matmul_mx(
                out=result[:],
                lhsT=w2_codes[:].bitcast(FP8X4),
                lhsT_scale=w2_plane[:],
                rhs=h_codes[:].bitcast(FP8X4),
                rhs_scale=h_plane[:],
                start=True,
                stop=True,
            )
            copy_out = nc.vector.tensor_copy if g == 2 else nc.scalar.copy
            copy_out(out=staged[:, lo:hi], in_=result[:])

        pick_and_add(2, 0, late)
        gelu_pair(0, CHUNK, HALF)
        gelu_pair(0, HALF, S)
        pick_and_add(3, 0, CHUNK)
        gelu_whole(0, CHUNK)
        for lo in (CHUNK, HALF):
            pick_and_add(3, lo, lo + CHUNK)
            gelu_pair(1, lo, lo + CHUNK)
        pick_and_add(2, late, S)
        for lo in (late, S - LAST):
            pick_and_add(3, lo, lo + LAST)
            gelu_pair(1, lo, lo + LAST)
        for g, (lo, hi) in enumerate(((0, CHUNK), (CHUNK, HALF), (HALF, late), (late, S - LAST), (S - LAST, S))):
            second_layer(g, lo, hi)
        for lo, hi in ((0, HALF), (HALF, late), (late, S)):
            nc.sync.dma_start(out=out[:, lo:hi], in_=staged[:, lo:hi])
